import numpy as np, ml_dtypes
CORES = [40,41,42,43,44,45,46,47]
N = 8
BF = ml_dtypes.bfloat16
def gentries(a):
    return np.ascontiguousarray(a.reshape(8, 16, -1).transpose(0, 2, 1)).reshape(8, -1)
def gtable(e):
    e = np.asarray(e); return np.ascontiguousarray(e.reshape(8, -1, 16).transpose(0, 2, 1)).reshape(128, -1).astype(np.int32)
M, Q, V, TOP = 1024, 512, 8, 31
WT = 15
def far_maps(rng):
    p = np.argsort(rng.random((N, 8, M)), axis=-1)
    return np.where(rng.random(p.shape) < 0.125, rng.integers(0, M, p.shape), p).astype(np.int32)
def lists(a):
    return np.stack([gtable(u) for u in a])
def setup_inputs(rng):
    return {"nx": far_maps(rng), "w": rng.integers(0, WT + 1, (N, 8, M)).astype(np.int32), "x": lists(rng.integers(0, M, (N, 8, Q))), "e": lists(rng.integers(0, TOP + 1, (N, 8, V * Q)))}
def setup_inputs_ends(rng):
    d = setup_inputs(rng); k = rng.choice(np.array([0, TOP]), (N, 8, V, Q))
    k[:, :, :, 0] = 0; k[:, :, :, 1] = TOP; k[:, :, :, Q - 1] = 0; k[:, :, V - 1, Q - 1] = TOP
    d["e"] = lists(k.reshape(N, 8, V * Q))
    w = np.where(rng.random((N, 8, M)) < 0.5, WT, 0); w[:, 0] = WT; d["w"] = w.astype(np.int32)
    return d
def setup_inputs_still(rng):
    d = setup_inputs(rng); a = np.array(d["nx"]); s = int(rng.integers(0, 4)); p = np.arange(M)
    for r in range(N):
        h = (r + s) % 4; c = rng.choice(np.arange(2, M - 1), 8, replace=False)
        if h == 0:
            a[r] = p
        elif h == 1:
            c[0] = 0; c[1] = M - 1; a[r] = rng.permutation(c)[:, None]
        elif h == 2:
            c[0] = 1; c[1] = M - 1; a[r] = (p + rng.permutation(c)[:, None]) % M
        else:
            c[0] = 1; c[1] = M - 1; a[r] = p ^ rng.permutation(c)[:, None]
    d["nx"] = a; return d
def setup_inputs_alike(rng):
    d = setup_inputs(rng); k = rng.integers(0, TOP + 1, (N, 8, V, Q // 2))
    z = np.where((np.arange(N)[:, None] + np.arange(8)) % 2 == 0, M - 1, 0)
    d["x"] = lists(np.repeat(z[:, :, None], Q, axis=2)); d["e"] = lists(np.concatenate([k, k], -1).reshape(N, 8, V * Q)); return d
def setup_inputs_spread(rng):
    d = setup_inputs(rng)
    d["nx"] = np.floor(M * rng.random((N, 8, M)) ** 3).astype(np.int32)
    d["w"] = np.floor((WT + 1) * rng.random((N, 8, M)) ** 4).astype(np.int32)
    d["x"] = lists(np.floor(M * rng.random((N, 8, Q)) ** 2)); d["e"] = lists(np.floor((TOP + 1) * rng.random((N, 8, V * Q)) ** 3)); return d
def check_inputs(d):
    bad = []
    for name, top in (("nx", M - 1), ("w", WT), ("x", M - 1), ("e", TOP)):
        if np.min(d[name]) < 0 or np.max(d[name]) > top: bad.append("range of " + name)
    return bad
def reference(nx, w, x, e):
    last = np.zeros((N, 128, Q // 16), np.int32); total = np.zeros((N, 128, Q // 16), np.int32); g = np.arange(8)[:, None]
    for r in range(N):
        p = gentries(x[r]).astype(np.int64); k = gentries(e[r]).reshape(8, V, Q); s = np.zeros((8, Q), np.int64)
        for t in range(V):
            q = (r + t) % N
            for i in range(TOP):
                go = i < k[:, t]
                s = s + np.where(go, w[q][g, p], 0)
                p = np.where(go, nx[q][g, p], p)
        last[r] = gtable(p); total[r] = gtable(s)
    return {"last": np.asarray(last, np.float32), "total": np.asarray(total, np.float32)}

@@ -1,0 +1,299 @@
+from concourse.bass import DstId, RemoteDMATransfer
+from concourse.mybir import AluOpType, ActivationFunctionType
+
+VC = 704
+SCRATCH = {"OH": ("sbuf", [128, 8], "float32"), "mk": ("sbuf", [128, 4096], "bfloat16")}
+for _n, _w in (("sm", 16), ("rm", 16), ("se", 32), ("rre", 32), ("sx", 4), ("rx", 4)):
+    SCRATCH[_n] = ("dram", [8, 128, _w], "int32")
+for _n in ("od", "ri"):
+    SCRATCH[_n] = ("dram", [8, 128, 8], "float32")
+for _d, _l in (("int32", "W0:1024 A1:1024 cmp:64 ei:256 xi:32 e7:256 li:256 hi:256 e70:32 li0:32 i1:256 pc:1 ci:16 da:256 db:256 dc:256 dd:256 jm:128"),
+               ("float32", "win:5120 W1:1024 W2:1024 adF:1024 OT:64 cf:16 mS:128 mb1:128 mb2:128 mb12:128 E15:128 BcF:128 ta:128 tb:128 tc:128 td:128 te:128 tf:128"),
+               ("float16", "g1:1024 g2:1024 g3:1024 ad16:1024 gb:1024 c16:64 y16:64 l16:256 h16:256 x16:32 G0:512 G1:512 Bc:128 C1:128 C2:128 D1:128 D2:128 D3:128 WI:256 WIe:256 WIo:256 WH:256 W7:256 WT:256 WS:256"),
+               ("uint16", "L1:64 L2:64 L4:64 L8:64 lu0:32 lu:256 off:32")):
+    for _e in _l.split():
+        SCRATCH[_e.split(":")[0]] = ("sbuf", [128, int(_e.split(":")[1])], _d)
+for _n in ("pR0", "pR1", "pM0", "pM1", "pN0", "pN1", "pA0", "pA1"):
+    SCRATCH[_n] = ("psum", [128, 512], "float32")
+SEMAPHORES = ["ld", "own", "ld2", "own2", "am", "ae", "ax", "cl", "wl", "xl", "v", "s", "p", "gi", "ls", "st", "own3", "ar", "fin"]
+
+
+def rank_program(g, core, T, topo):
+    me = T.rank_of(core)
+    if me is None:
+        return
+    V, S, P, Y = g.vector, g.scalar, g.tensor, g.sync
+    A = AluOpType
+    N = len(T.cores)
+    others = [(me + d) % N for d in range(1, N)]
+    sem = T.sem
+    cnt = {"v": 0, "s": 0, "p": 0, "gi": 0}
+    seen = {}
+    queues = {"v": V, "s": S, "p": P, "g": g, "y": Y}
+
+    def wait(q, *toks):
+        for name, n in toks:
+            if n > seen.get((q, name), 0):
+                queues[q].wait_ge(sem[name], n)
+                seen[(q, name)] = n
+
+    def done(name, ins):
+        cnt[name] += 1
+        ins.then_inc(sem[name], 1)
+        return (name, cnt[name])
+
+    def copyV(out, in_, *w):
+        wait("v", *w)
+        return done("v", V.tensor_copy(out=out, in_=in_))
+
+    def tsV(out, in0, s1, op0, *w, s2=None, op1=None):
+        wait("v", *w)
+        if op1 is None:
+            return done("v", V.tensor_scalar(out=out, in0=in0, scalar1=s1, scalar2=None, op0=op0))
+        return done("v", V.tensor_scalar(out=out, in0=in0, scalar1=s1, scalar2=s2, op0=op0, op1=op1))
+
+    def ttV(out, in0, in1, op, *w):
+        wait("v", *w)
+        return done("v", V.tensor_tensor(out=out, in0=in0, in1=in1, op=op))
+
+    def copyS(out, in_, *w):
+        wait("s", *w)
+        return done("s", S.activation(out=out, in_=in_, func=ActivationFunctionType.Copy))
+
+    def mm(out, lhsT, rhs, start, stop, *w):
+        wait("p", *w)
+        ins = P.matmul(out=out, lhsT=lhsT, rhs=rhs, start=start, stop=stop)
+        return done("p", ins) if stop else None
+
+    def fused(src, dst, rsem):
+        tr = []
+        for n, d in enumerate(others):
+            c = T.cores[d]
+            rid, pid, _ = topo.addr(c)
+            eng = topo.engines(core, c)
+            e = eng[(2 * n) % len(eng)]
+            tr.append(RemoteDMATransfer(src=src[d], dst=dst[me], dst_ids=[DstId(rid=rid, pnc=pid)], dma_engine_mask=1 << e, remote_sem=sem[rsem]))
+        g.remote_dma_fused(tr, local_sem=sem.ls)
+
+    mine = slice(16 * me, 16 * me + 16)
+    for q, out, in_, name in ((Y, T.sm[:, 0:64, :], T.nx[:, :], "ld"), (S, T.sm[:, 64:128, :], T.w[:, :], "ld"),
+                              (Y, T.se[:], T.e[:, :], "ld2"), (S, T.sx[:], T.x[:, :], "ld2"),
+                              (Y, T.rm[me, 0:64, :], T.nx[me, :], "own"), (S, T.rm[me, 64:128, :], T.w[me, :], "own"),
+                              (Y, T.rre[me], T.e[mine, :], "own2"), (S, T.rx[me], T.x[mine, :], "own2")):
+        q.dma_start(out=out, in_=in_).then_inc(sem[name], 16)
+
+    k_pc = done("gi", g.iota(T.pc[:, 0:1], [[0, 1]], 0, 1))
+    k_i1 = done("gi", g.iota(T.i1[:], [[1, 256]], 128, 0))
+    g.wait_ge(sem.ld, 32)
+    fused(T.sm, T.rm, "am")
+    g.wait_ge(sem.ld2, 32)
+    fused(T.se, T.rre, "ae")
+    fused(T.sx, T.rx, "ax")
+    for buf, pat in ((T.mS, [[0, 8], [1, 2], [0, 8]]), (T.mb1, [[0, 32], [1, 2], [0, 2]]), (T.mb2, [[0, 16], [1, 2], [0, 4]])):
+        k_fl = done("gi", g.iota(buf[:], pat, 0, 0, allow_small_or_imprecise_dtypes=True))
+
+    names = ["T", "S", "7", "15", "q", "p", "he", "ho", "b1", "n1", "b2", "n2", "k7"]
+    col = {n: T.cf[:, i:i + 1] for i, n in enumerate(names)}
+    c15, c112, c16b, cb1, cb2, ck7 = [T.ci[:, i:i + 1] for i in range(6)]
+    wait("v", k_pc)
+    for c, bits in ((c15, 15), (c112, 112), (c16b, 16), (cb1, 2), (cb2, 4), (ck7, 7)):
+        kc = tsV(c, T.pc[:, 0:1], bits, A.bitwise_and)
+    k_a1 = done("v", V.memset(T.A1[:], 0))
+    kT = tsV(col["T"], c15, 8.0, A.is_lt, kc)
+    for n, c, x in (("S", c15, 8.0), ("7", c15, 7.0), ("15", c15, 15.0), ("he", c16b, 0.0), ("ho", c16b, 16.0),
+                    ("b1", cb1, 2.0), ("n1", cb1, 0.0), ("b2", cb2, 4.0), ("n2", cb2, 0.0)):
+        tsV(col[n], c, x, A.is_ge if n == "S" else A.is_equal)
+    copyV(col["q"], c112)
+    copyV(col["k7"], ck7)
+    kcol = copyV(col["p"], T.pc[:, 0:1])
+    for i in range(4):
+        k_w0 = tsV(T.W0[:, 256 * i:256 * i + 256], T.i1[:], float(256 * i - 128), A.add, k_i1, kT, s2=col["T"], op1=A.mult)
+    k1 = tsV(T.da[:], T.i1[:], col["p"], A.subtract, kcol)
+    k2 = tsV(T.dc[:], T.i1[:], col["q"], A.subtract)
+    k3 = tsV(T.db[:], T.da[:], 127, A.bitwise_and, k1)
+    k4 = tsV(T.dd[:], T.dc[:], 127, A.bitwise_and, k2)
+    tsV(T.WIe[:], T.db[:], 0.0, A.is_equal, k3, s2=col["he"], op1=A.mult)
+    k_wio = tsV(T.WIo[:], T.db[:], 0.0, A.is_equal, s2=col["ho"], op1=A.mult)
+    k_w7 = tsV(T.W7[:], T.dd[:], 0.0, A.is_equal, k4, s2=col["7"], op1=A.mult)
+    kI = tsV(T.WI[:], T.db[:], 0.0, A.is_equal)
+    I = T.WI[:, 0:128]
+    kj = tsV(T.jm[:], T.i1[:, 0:128], 112, A.bitwise_and)
+    kE = tsV(T.E15[:], T.jm[:], col["q"], A.is_equal, kj, s2=col["15"], op1=A.mult)
+    kb = ttV(T.BcF[:], T.E15[:], T.mS[:], A.mult, kE, k_fl)
+    k12 = ttV(T.mb12[:], T.mb1[:], T.mb2[:], A.max)
+    tsV(T.C2[:], I, col["b1"], A.mult, kI)
+    tsV(T.D3[:], I, col["b2"], A.mult)
+    tsV(T.ta[:], I, col["n1"], A.mult)
+    tsV(T.tb[:], I, col["n2"], A.mult, s2=col["n1"], op1=A.mult)
+    tsV(T.tc[:], I, col["n2"], A.mult, s2=col["b1"], op1=A.mult)
+    ttV(T.td[:], T.BcF[:], T.mb1[:], A.mult, kb)
+    ttV(T.te[:], T.BcF[:], T.mb12[:], A.mult, k12)
+    kt = ttV(T.tf[:], T.BcF[:], T.mb2[:], A.mult)
+    ttV(T.C1[:], T.ta[:], T.td[:], A.add, kt)
+    ttV(T.D1[:], T.tb[:], T.te[:], A.add)
+    ttV(T.D2[:], T.tc[:], T.tf[:], A.add)
+    k_mat = copyV(T.Bc[:], T.BcF[:])
+    tsV(T.WT[:], T.dd[:], 0.0, A.is_equal, s2=col["T"], op1=A.mult)
+    tsV(T.WS[:], T.dd[:], 0.0, A.is_equal, s2=col["S"], op1=A.mult)
+    tsV(T.WH[:], T.db[:], 0.0, A.is_equal, s2=128.0, op1=A.mult)
+    tsV(T.OH[:], T.i1[:, 0:8], col["k7"], A.subtract, s2=128.0, op1=A.is_equal)
+    for i in range(4):
+        k_late = tsV(T.win[:, 256 * i:256 * i + 256], T.i1[:], float(256 * i - 128), A.add, s2=col["T"], op1=A.mult)
+
+    nxl, wl = T.rm[:, 0:64, :], T.rm[:, 64:128, :]
+    for e in (Y, S):
+        e.wait_ge(sem.own, 32)
+        e.wait_ge(sem.am, N - 1)
+    Y.dma_start(out=T.cmp[:], in_=nxl).then_inc(sem.cl, 16)
+    wait("y", k_a1, k_w0)
+    wait("s", k_a1, k_w0)
+    for k in (1, 3, 5, 7):
+        Y.dma_start(out=T.W0[k::16, :], in_=nxl).then_inc(sem.wl, 16)
+        S.dma_start(out=T.W0[8 + k::16, :], in_=wl).then_inc(sem.wl, 16)
+    for k in (8, 10, 12, 14):
+        Y.dma_start(out=T.A1[k::16, :], in_=wl).then_inc(sem.wl, 16)
+        S.dma_start(out=T.A1[k + 1::16, :], in_=wl).then_inc(sem.wl, 16)
+    Y.wait_ge(sem.own2, 32)
+    Y.wait_ge(sem.ae, N - 1)
+    Y.dma_start(out=T.ei[:], in_=T.rre[:]).then_inc(sem.xl, 16)
+    Y.wait_ge(sem.ax, N - 1)
+    Y.dma_start(out=T.xi[:], in_=T.rx[:]).then_inc(sem.xl, 16)
+
+    wait("v", ("cl", 16))
+    k = copyV(T.c16[:], T.cmp[:])
+    wait("v", k)
+    k = done("v", V.transpose(out=T.y16[:], in_=T.c16[:]))
+    wait("p", k, k_wio)
+    for b in range(2):
+        for h0 in range(2):
+            for h in range(2):
+                s = 0 if h == h0 else (112 if h == 1 else 16)
+                c = 32 * b + 16 * h
+                kL = mm(T.pR1[:, 2 * b + h0:64:4], (T.WIe, T.WIo)[h0][:, s:s + 128], T.y16[:, c:c + 16], h == 0, h == 1)
+    kL1 = copyV(T.L1[:], T.pR1[:, 0:64], kL)
+
+    def relay(bank, wide, src, shift, n, first, *w):
+        wait("p", *w)
+        for r in range(16):
+            s = (shift - r) % 128
+            k = mm(bank[:, 0:n], wide[:, s:s + 128], src[:, r::16], first and r == 0, r == 15)
+        return k
+
+    H = (slice(0, 512), slice(512, 1024))
+    wait("v", ("wl", 256))
+    kg1 = [ttV(T.g1[:, H[h]], T.W0[:].indirect(T.L1[:, 32 * h:32 * h + 32]), T.A1[:, H[h]], A.add, kL1) for h in range(2)]
+    kr = relay(T.pR0, T.W7, T.g1, 0, 64, True, k_w7, *kg1)
+    copyS(T.W1[:, 0:512], T.g1[:, 0:512], kg1[0])
+    ks1 = copyS(T.W1[:, 512:768], T.g1[:, 512:768], kg1[1])
+    kv1 = copyV(T.W1[:, 768:1024], T.g1[:, 768:1024], kg1[1])
+    kl = copyV(T.L2[:], T.pR0[:, 0:64], kr)
+
+    pM, pN, pA = (T.pM0, T.pM1), (T.pN0, T.pN1), (T.pA0, T.pA1)
+    wait("p", k_mat)
+    for h in range(2):
+        mm(pM[h][:], T.C1[:], T.g1[:, H[h]], True, False)
+    for h in range(2):
+        mm(pN[h][:], T.D1[:], T.g1[:, H[h]], True, False)
+    kg2v = copyV(T.g2[:, H[0]], T.W1[:].indirect(T.L2[:, 0:32]), kl, ks1, kv1)
+    kg2s = copyS(T.g2[:, H[1]], T.W1[:].indirect(T.L2[:, 32:64]), kl, ks1, kv1)
+    m0 = mm(pM[0][:], T.C2[:], T.g2[:, H[0]], False, True, kg2v)
+    m1 = mm(pM[1][:], T.C2[:], T.g2[:, H[1]], False, True, kg2s)
+    kr = relay(T.pR1, T.W7, T.g2, 0, 64, True, kL1)
+    kw2v = copyV(T.W2[:, H[0]], pM[0][:], m0)
+    kw2s = copyS(T.W2[:, H[1]], pM[1][:], m1)
+    kl = copyV(T.L4[:], T.pR1[:, 0:64], kr)
+
+    for h in range(2):
+        mm(pN[h][:], T.D2[:], T.g2[:, H[h]], False, False)
+    for h in range(2):
+        mm(pA[h][:], T.Bc[:], T.g1[:, H[h]], True, False)
+    kg3v = copyV(T.g3[:, H[0]], T.W2[:].indirect(T.L4[:, 0:32]), kl, kw2v, kw2s)
+    kg3s = copyS(T.g3[:, H[1]], T.W2[:].indirect(T.L4[:, 32:64]), kl, kw2v, kw2s)
+    m0 = mm(pN[0][:], T.D3[:], T.g3[:, H[0]], False, True, kg3v)
+    m1 = mm(pN[1][:], T.D3[:], T.g3[:, H[1]], False, True, kg3s)
+    kr = relay(T.pR0, T.W7, T.g3, 0, 64, True, kl)
+    kad = []
+    for h in range(2):
+        mm(pA[h][:], T.Bc[:], T.g2[:, H[h]], False, False)
+        kad.append(mm(pA[h][:], T.Bc[:], T.g3[:, H[h]], False, True))
+    kb1v = copyV(T.win[:, 1024:1536], pN[0][:], m0)
+    kb1s = copyS(T.win[:, 1536:2048], pN[1][:], m1)
+    wait("v", ("xl", 32))
+    k = tsV(T.e70[:], T.ei[:, 0:32], 7.0, A.add)
+    k = tsV(T.li0[:], T.e70[:], 7, A.bitwise_and, k)
+    klu0 = copyV(T.lu0[:], T.li0[:], k)
+    kl8 = copyV(T.L8[:], T.pR0[:, 0:64], kr)
+    kmask = [copyS(T.mk[:, 0:512], T.OH[:].indirect(T.lu0[:]), klu0, k_late)]
+
+    k = tsV(T.e7[:], T.ei[:], 7.0, A.add)
+    k5 = tsV(T.li[:], T.e7[:], 7, A.bitwise_and, k)
+    k6 = tsV(T.hi[:], T.e7[:], 56, A.bitwise_and)
+    k5 = copyV(T.l16[:], T.li[:], k5)
+    k6 = copyV(T.h16[:], T.hi[:], k6)
+    k7 = copyV(T.x16[:], T.xi[:])
+    kadV = copyV(T.adF[:, 0:512], pA[0][:], kad[0])
+    kadS = copyS(T.adF[:, 512:VC], pA[1][:, 0:VC - 512], kad[1])
+    kadT = copyS(T.ad16[:, VC:1024], pA[1][:, VC - 512:512], kad[1])
+    wait("p", k5, k6, k7, k_late)
+    for t in range(8):
+        s = (128 - 16 * t) % 128
+        kt = mm(T.pM1[:, 32 * t:32 * t + 32], T.WI[:, s:s + 128], T.l16[:, 32 * t:32 * t + 32], True, True, kw2s)
+    mm(T.pR1[:, 0:32], I, T.x16[:], True, False, kl)
+    ko = mm(T.pR1[:, 0:32], T.WH[:, 0:128], T.h16[:, 0:32], False, True)
+    klu = copyV(T.lu[:], T.pM1[:, 0:256], kt)
+    koff = copyV(T.off[:], T.pR1[:, 0:32], ko)
+
+    nS = 1024 - VC
+    kprev = [kb1v, kb1s]
+    kps = [kb1v, kb1s]
+    for B in range(2, 5):
+        a = 1024 * (B - 1)
+        src = T.win[:, a:a + 1024]
+        bank = pN[B % 2]
+        kv = ttV(T.win[:, a + 1024:a + 1024 + VC], src.indirect(T.L8[:, 0:VC // 16]), T.adF[:, 0:VC], A.add, kl8, kadS, kadV, *kprev)
+        kg = copyS(T.gb[:, VC:1024], src.indirect(T.L8[:, VC // 16:64]), kl8, kadT, *kprev)
+        mm(bank[:, 0:nS], I, T.ad16[:, VC:1024], True, False, kadT, *kps)
+        km = mm(bank[:, 0:nS], I, T.gb[:, VC:1024], False, True, kg)
+        ks = copyS(T.win[:, a + 1024 + VC:a + 2048], bank[:, 0:nS], km)
+        kprev = [kv, ks]
+        kps = [ks]
+    for t in range(1, 8):
+        kmask.append(copyS(T.mk[:, 512 * t:512 * t + 512], T.OH[:].indirect(T.lu[:, 32 * t:32 * t + 32]), klu))
+
+    ksum = {}
+    for t in range(8):
+        G, bank = (T.G0, T.G1)[t % 2], (T.pR0, T.pR1)[t % 2]
+        if t > 1:
+            wait("v", ksum[t - 2])
+        kg = ttV(G[:], T.win[:].indirect(T.off[:]), T.mk[:, 512 * t:512 * t + 512], A.mult, koff, kmask[t], *kprev)
+        if t < 7:
+            s = (128 - 16 * (t + 1)) % 128
+            mm(bank[:, 0:32], T.WH[:, s:s + 128], T.h16[:, 32 * (t + 1):32 * (t + 2)], True, False, kl8, koff)
+        kr = relay(bank, T.WT, G, 112, 32, t == 7, kg, koff)
+        if t < 7:
+            koff = copyV(T.off[:], bank[:, 0:32], kr)
+        else:
+            klast = copyV(T.OT[:, 0:32], bank[:, 0:32], kr)
+        for r in range(16):
+            s = (16 * t - r) % 128
+            wait("p", kw2v)
+            ins = P.matmul(out=T.pM0[:, 0:32], lhsT=T.WS[:, s:s + 128], rhs=G[:, r::16], start=(t == 0 and r == 0), stop=(t == 7 and r == 15))
+        ksum[t] = done("p", ins)
+    ktot = copyS(T.OT[:, 32:64], T.pM0[:, 0:32], ksum[7])
+
+    wait("y", klast)
+    Y.dma_start(out=T.od[:, 0:64, :], in_=T.OT[:, 0:32]).then_inc(sem.st, 16)
+    Y.dma_start(out=T.ri[me, 0:64, :], in_=T.OT[mine, 0:32]).then_inc(sem.own3, 16)
+    wait("s", ktot)
+    S.dma_start(out=T.od[:, 64:128, :], in_=T.OT[:, 32:64]).then_inc(sem.st, 16)
+    S.dma_start(out=T.ri[me, 64:128, :], in_=T.OT[mine, 32:64]).then_inc(sem.own3, 16)
+    g.wait_ge(sem.st, 32)
+    fused(T.od, T.ri, "ar")
+    for e in (Y, S):
+        e.wait_ge(sem.own3, 32)
+        e.wait_ge(sem.ar, N - 1)
+    Y.dma_start(out=T.last[:, :], in_=T.ri[:, 0:64, :]).then_inc(sem.fin, 16)
+    S.dma_start(out=T.total[:, :], in_=T.ri[:, 64:128, :]).then_inc(sem.fin, 16)
+    wait("g", ("v", cnt["v"]), ("s", cnt["s"]), ("p", cnt["p"]), ("gi", cnt["gi"]))
+    g.wait_ge(sem.ls, 4 * (N - 1))
+    g.wait_ge(sem.fin, 32)

@@ -7,9 +7,9 @@ for _n, _w in (("sm", 16), ("rm", 16), ("se", 32), ("rre", 32), ("sx", 4), ("rx"
     SCRATCH[_n] = ("dram", [8, 128, _w], "int32")
 for _n in ("od", "ri"):
     SCRATCH[_n] = ("dram", [8, 128, 8], "float32")
-for _d, _l in (("int32", "W0:1024 A1:1024 cmp:64 ei:256 xi:32 e7:256 li:256 hi:256 e70:32 li0:32 i1:256 pc:1 ci:16 da:256 db:256 dc:256 dd:256 jm:128"),
-               ("float32", "win:5120 W1:1024 W2:1024 adF:1024 OT:64 cf:16 mS:128 mb1:128 mb2:128 mb12:128 E15:128 BcF:128 ta:128 tb:128 tc:128 td:128 te:128 tf:128"),
-               ("float16", "g1:1024 g2:1024 g3:1024 ad16:1024 gb:1024 c16:64 y16:64 l16:256 h16:256 x16:32 G0:512 G1:512 Bc:128 C1:128 C2:128 D1:128 D2:128 D3:128 WI:256 WIe:256 WIo:256 WH:256 W7:256 WT:256 WS:256"),
+for _d, _l in (("int32", "W0:1024 A1:1024 cmp:64 ei:256 xi:32 e7:256 li:256 hi:256 e70:32 li0:32 i1:256 pc:1 ci:8 da:256 db:256"),
+               ("float32", "win:5120 W1:1024 W2:1024 adF:1024 OT:64 cf:24"),
+               ("float16", "g1:1024 g2:1024 g3:1024 ad16:1024 gb:1024 c16:64 y16:64 l16:256 h16:256 x16:32 G0:512 G1:512 B9:128 B11:128 C1:128 C2:128 D1:128 D2:128 D3:128 WI:256 WIe:256 WIo:256 WH:256 W1r:256 W3r:256 Wb:256 WT:256 WS:256"),
                ("uint16", "L1:64 L2:64 L4:64 L8:64 lu0:32 lu:256 off:32")):
     for _e in _l.split():
         SCRATCH[_e.split(":")[0]] = ("sbuf", [128, int(_e.split(":")[1])], _d)
@@ -24,6 +24,7 @@ def rank_program(g, core, T, topo):
         return
     V, S, P, Y = g.vector, g.scalar, g.tensor, g.sync
     A = AluOpType
+    COPY = ActivationFunctionType.Copy
     N = len(T.cores)
     others = [(me + d) % N for d in range(1, N)]
     sem = T.sem
@@ -56,9 +57,9 @@ def rank_program(g, core, T, topo):
         wait("v", *w)
         return done("v", V.tensor_tensor(out=out, in0=in0, in1=in1, op=op))
 
-    def copyS(out, in_, *w):
+    def copyS(out, in_, *w, scale=1.0):
         wait("s", *w)
-        return done("s", S.activation(out=out, in_=in_, func=ActivationFunctionType.Copy))
+        return done("s", S.activation(out=out, in_=in_, func=COPY, scale=scale))
 
     def mm(out, lhsT, rhs, start, stop, *w):
         wait("p", *w)
@@ -89,56 +90,54 @@ def rank_program(g, core, T, topo):
     g.wait_ge(sem.ld2, 32)
     fused(T.se, T.rre, "ae")
     fused(T.sx, T.rx, "ax")
-    for buf, pat in ((T.mS, [[0, 8], [1, 2], [0, 8]]), (T.mb1, [[0, 32], [1, 2], [0, 2]]), (T.mb2, [[0, 16], [1, 2], [0, 4]])):
-        k_fl = done("gi", g.iota(buf[:], pat, 0, 0, allow_small_or_imprecise_dtypes=True))
+    k_id = done("gi", g.iota(T.win[:, 0:1024], [[1, 1024]], 0, 0, allow_small_or_imprecise_dtypes=True))
 
-    names = ["T", "S", "7", "15", "q", "p", "he", "ho", "b1", "n1", "b2", "n2", "k7"]
+    names = ["T", "S", "p", "he", "ho", "r1", "r3", "r9", "r11", "R01", "R03", "uC", "u1", "u2", "u9", "u11", "neg", "k7"]
     col = {n: T.cf[:, i:i + 1] for i, n in enumerate(names)}
-    c15, c112, c16b, cb1, cb2, ck7 = [T.ci[:, i:i + 1] for i in range(6)]
-    wait("v", k_pc)
-    for c, bits in ((c15, 15), (c112, 112), (c16b, 16), (cb1, 2), (cb2, 4), (ck7, 7)):
-        kc = tsV(c, T.pc[:, 0:1], bits, A.bitwise_and)
+    c15, c7, c16b, cn, cn7 = [T.ci[:, i:i + 1] for i in range(5)]
     k_a1 = done("v", V.memset(T.A1[:], 0))
+    wait("v", k_pc)
+    tsV(c15, T.pc[:, 0:1], 15, A.bitwise_and)
+    tsV(c7, T.pc[:, 0:1], 7, A.bitwise_and)
+    kc = tsV(c16b, T.pc[:, 0:1], 16, A.bitwise_and)
+    kp = copyV(col["p"], T.pc[:, 0:1])
     kT = tsV(col["T"], c15, 8.0, A.is_lt, kc)
-    for n, c, x in (("S", c15, 8.0), ("7", c15, 7.0), ("15", c15, 15.0), ("he", c16b, 0.0), ("ho", c16b, 16.0),
-                    ("b1", cb1, 2.0), ("n1", cb1, 0.0), ("b2", cb2, 4.0), ("n2", cb2, 0.0)):
-        tsV(col[n], c, x, A.is_ge if n == "S" else A.is_equal)
-    copyV(col["q"], c112)
-    copyV(col["k7"], ck7)
-    kcol = copyV(col["p"], T.pc[:, 0:1])
+    tsV(col["he"], c16b, 0.0, A.is_equal)
+    tsV(col["ho"], c16b, 16.0, A.is_equal)
+    kr1 = tsV(col["r1"], c15, 1.0, A.is_equal)
+    k = tsV(T.da[:], T.i1[:], col["p"], A.subtract, k_i1, kp)
+    k_db = tsV(T.db[:], T.da[:], 127, A.bitwise_and, k)
     for i in range(4):
-        k_w0 = tsV(T.W0[:, 256 * i:256 * i + 256], T.i1[:], float(256 * i - 128), A.add, k_i1, kT, s2=col["T"], op1=A.mult)
-    k1 = tsV(T.da[:], T.i1[:], col["p"], A.subtract, kcol)
-    k2 = tsV(T.dc[:], T.i1[:], col["q"], A.subtract)
-    k3 = tsV(T.db[:], T.da[:], 127, A.bitwise_and, k1)
-    k4 = tsV(T.dd[:], T.dc[:], 127, A.bitwise_and, k2)
-    tsV(T.WIe[:], T.db[:], 0.0, A.is_equal, k3, s2=col["he"], op1=A.mult)
+        k_w0 = tsV(T.W0[:, 256 * i:256 * i + 256], T.i1[:], float(256 * i - 128), A.add, kT, s2=col["T"], op1=A.mult)
+    tsV(T.WIe[:], T.db[:], 0.0, A.is_equal, k_db, kr1, s2=col["he"], op1=A.mult)
     k_wio = tsV(T.WIo[:], T.db[:], 0.0, A.is_equal, s2=col["ho"], op1=A.mult)
-    k_w7 = tsV(T.W7[:], T.dd[:], 0.0, A.is_equal, k4, s2=col["7"], op1=A.mult)
-    kI = tsV(T.WI[:], T.db[:], 0.0, A.is_equal)
+    k_w1r = tsV(T.W1r[:], T.db[:], 127.0, A.is_equal, s2=col["r1"], op1=A.mult)
+    tsV(col["R01"], c7, 2.0, A.is_lt)
+    tsV(col["R03"], c7, 4.0, A.is_lt)
+    tsV(col["r11"], c15, 11.0, A.is_equal)
+    tsV(col["r3"], c15, 3.0, A.is_equal)
+    tsV(col["S"], c15, 8.0, A.is_ge)
+    k = tsV(col["r9"], c15, 9.0, A.is_equal)
+    for n, f in (("uC", 2.0), ("u1", 6.0), ("u2", 4.0)):
+        tsV(col[n], col["r9"], f, A.mult, k, s2=col["R01"], op1=A.add)
+    tsV(col["u9"], col["r9"], 8.0, A.mult)
+    k = tsV(col["u11"], col["r11"], 8.0, A.mult)
+    tsV(T.C1[:], T.db[:, 0:128], col["uC"], A.is_lt, k)
+    tsV(T.C2[:], T.db[:, 0:128], 2.0, A.is_equal, s2=col["R01"], op1=A.mult)
+    tsV(T.D1[:], T.db[:, 0:128], col["u1"], A.is_lt)
+    tsV(T.D2[:], T.db[:, 126:254], col["u2"], A.is_lt)
+    tsV(T.D3[:], T.db[:, 0:128], 4.0, A.is_equal, s2=col["R03"], op1=A.mult)
+    tsV(T.B9[:], T.db[:, 1:129], col["u9"], A.is_lt)
+    tsV(T.B11[:], T.db[:, 3:131], col["u11"], A.is_lt)
+    k_mat = tsV(T.WI[:], T.db[:], 0.0, A.is_equal)
     I = T.WI[:, 0:128]
-    kj = tsV(T.jm[:], T.i1[:, 0:128], 112, A.bitwise_and)
-    kE = tsV(T.E15[:], T.jm[:], col["q"], A.is_equal, kj, s2=col["15"], op1=A.mult)
-    kb = ttV(T.BcF[:], T.E15[:], T.mS[:], A.mult, kE, k_fl)
-    k12 = ttV(T.mb12[:], T.mb1[:], T.mb2[:], A.max)
-    tsV(T.C2[:], I, col["b1"], A.mult, kI)
-    tsV(T.D3[:], I, col["b2"], A.mult)
-    tsV(T.ta[:], I, col["n1"], A.mult)
-    tsV(T.tb[:], I, col["n2"], A.mult, s2=col["n1"], op1=A.mult)
-    tsV(T.tc[:], I, col["n2"], A.mult, s2=col["b1"], op1=A.mult)
-    ttV(T.td[:], T.BcF[:], T.mb1[:], A.mult, kb)
-    ttV(T.te[:], T.BcF[:], T.mb12[:], A.mult, k12)
-    kt = ttV(T.tf[:], T.BcF[:], T.mb2[:], A.mult)
-    ttV(T.C1[:], T.ta[:], T.td[:], A.add, kt)
-    ttV(T.D1[:], T.tb[:], T.te[:], A.add)
-    ttV(T.D2[:], T.tc[:], T.tf[:], A.add)
-    k_mat = copyV(T.Bc[:], T.BcF[:])
-    tsV(T.WT[:], T.dd[:], 0.0, A.is_equal, s2=col["T"], op1=A.mult)
-    tsV(T.WS[:], T.dd[:], 0.0, A.is_equal, s2=col["S"], op1=A.mult)
-    tsV(T.WH[:], T.db[:], 0.0, A.is_equal, s2=128.0, op1=A.mult)
+    tsV(T.W3r[:], T.db[:], 125.0, A.is_equal, s2=col["r3"], op1=A.mult)
+    k = tsV(cn, c15, -1.0, A.mult, s2=128.0, op1=A.add)
+    copyV(col["k7"], c7)
+    k = tsV(cn7, cn, 127, A.bitwise_and, k)
+    k = copyV(col["neg"], cn7, k)
     tsV(T.OH[:], T.i1[:, 0:8], col["k7"], A.subtract, s2=128.0, op1=A.is_equal)
-    for i in range(4):
-        k_late = tsV(T.win[:, 256 * i:256 * i + 256], T.i1[:], float(256 * i - 128), A.add, s2=col["T"], op1=A.mult)
+    k_wb = tsV(T.Wb[:], T.db[:], col["neg"], A.is_equal, k)
 
     nxl, wl = T.rm[:, 0:64, :], T.rm[:, 64:128, :]
     for e in (Y, S):
@@ -147,17 +146,19 @@ def rank_program(g, core, T, topo):
     Y.dma_start(out=T.cmp[:], in_=nxl).then_inc(sem.cl, 16)
     wait("y", k_a1, k_w0)
     wait("s", k_a1, k_w0)
-    for k in (1, 3, 5, 7):
-        Y.dma_start(out=T.W0[k::16, :], in_=nxl).then_inc(sem.wl, 16)
-        S.dma_start(out=T.W0[8 + k::16, :], in_=wl).then_inc(sem.wl, 16)
-    for k in (8, 10, 12, 14):
-        Y.dma_start(out=T.A1[k::16, :], in_=wl).then_inc(sem.wl, 16)
-        S.dma_start(out=T.A1[k + 1::16, :], in_=wl).then_inc(sem.wl, 16)
+    S.dma_start(out=T.W0[9::16, :], in_=wl).then_inc(sem.wl, 16)
+    Y.dma_start(out=T.W0[1::16, :], in_=nxl).then_inc(sem.wl, 16)
+    S.dma_start(out=T.A1[9::16, :], in_=wl).then_inc(sem.wl, 16)
+    Y.dma_start(out=T.A1[8::16, :], in_=wl).then_inc(sem.wl, 16)
     Y.wait_ge(sem.own2, 32)
     Y.wait_ge(sem.ae, N - 1)
     Y.dma_start(out=T.ei[:], in_=T.rre[:]).then_inc(sem.xl, 16)
     Y.wait_ge(sem.ax, N - 1)
     Y.dma_start(out=T.xi[:], in_=T.rx[:]).then_inc(sem.xl, 16)
+    copyS(T.WH[:], T.WI[:], k_mat, scale=128.0)
+    copyS(T.WT[:], T.Wb[:], k_wb, scale=col["T"])
+    copyS(T.WS[:], T.Wb[:], scale=col["S"])
+    k_late = copyS(T.win[:, 0:1024], T.win[:, 0:1024], k_id, scale=col["T"])
 
     wait("v", ("cl", 16))
     k = copyV(T.c16[:], T.cmp[:])
@@ -180,9 +181,9 @@ def rank_program(g, core, T, topo):
         return k
 
     H = (slice(0, 512), slice(512, 1024))
-    wait("v", ("wl", 256))
+    wait("v", ("wl", 64))
     kg1 = [ttV(T.g1[:, H[h]], T.W0[:].indirect(T.L1[:, 32 * h:32 * h + 32]), T.A1[:, H[h]], A.add, kL1) for h in range(2)]
-    kr = relay(T.pR0, T.W7, T.g1, 0, 64, True, k_w7, *kg1)
+    kr = relay(T.pR0, T.W1r, T.g1, 0, 64, True, k_w1r, *kg1)
     copyS(T.W1[:, 0:512], T.g1[:, 0:512], kg1[0])
     ks1 = copyS(T.W1[:, 512:768], T.g1[:, 512:768], kg1[1])
     kv1 = copyV(T.W1[:, 768:1024], T.g1[:, 768:1024], kg1[1])
@@ -198,7 +199,7 @@ def rank_program(g, core, T, topo):
     kg2s = copyS(T.g2[:, H[1]], T.W1[:].indirect(T.L2[:, 32:64]), kl, ks1, kv1)
     m0 = mm(pM[0][:], T.C2[:], T.g2[:, H[0]], False, True, kg2v)
     m1 = mm(pM[1][:], T.C2[:], T.g2[:, H[1]], False, True, kg2s)
-    kr = relay(T.pR1, T.W7, T.g2, 0, 64, True, kL1)
+    kr = relay(T.pR1, T.W1r, T.g2, 0, 64, True, kL1)
     kw2v = copyV(T.W2[:, H[0]], pM[0][:], m0)
     kw2s = copyS(T.W2[:, H[1]], pM[1][:], m1)
     kl = copyV(T.L4[:], T.pR1[:, 0:64], kr)
@@ -206,16 +207,16 @@ def rank_program(g, core, T, topo):
     for h in range(2):
         mm(pN[h][:], T.D2[:], T.g2[:, H[h]], False, False)
     for h in range(2):
-        mm(pA[h][:], T.Bc[:], T.g1[:, H[h]], True, False)
+        mm(pA[h][:], T.B9[:], T.g1[:, H[h]], True, False)
     kg3v = copyV(T.g3[:, H[0]], T.W2[:].indirect(T.L4[:, 0:32]), kl, kw2v, kw2s)
     kg3s = copyS(T.g3[:, H[1]], T.W2[:].indirect(T.L4[:, 32:64]), kl, kw2v, kw2s)
     m0 = mm(pN[0][:], T.D3[:], T.g3[:, H[0]], False, True, kg3v)
     m1 = mm(pN[1][:], T.D3[:], T.g3[:, H[1]], False, True, kg3s)
-    kr = relay(T.pR0, T.W7, T.g3, 0, 64, True, kl)
+    kr = relay(T.pR0, T.W3r, T.g3, 0, 64, True, kl, k_wb)
     kad = []
     for h in range(2):
-        mm(pA[h][:], T.Bc[:], T.g2[:, H[h]], False, False)
-        kad.append(mm(pA[h][:], T.Bc[:], T.g3[:, H[h]], False, True))
+        mm(pA[h][:], T.B9[:], T.g2[:, H[h]], False, False)
+        kad.append(mm(pA[h][:], T.B11[:], T.g3[:, H[h]], False, True))
     kb1v = copyV(T.win[:, 1024:1536], pN[0][:], m0)
     kb1s = copyS(T.win[:, 1536:2048], pN[1][:], m1)
     wait("v", ("xl", 32))
@@ -223,7 +224,7 @@ def rank_program(g, core, T, topo):
     k = tsV(T.li0[:], T.e70[:], 7, A.bitwise_and, k)
     klu0 = copyV(T.lu0[:], T.li0[:], k)
     kl8 = copyV(T.L8[:], T.pR0[:, 0:64], kr)
-    kmask = [copyS(T.mk[:, 0:512], T.OH[:].indirect(T.lu0[:]), klu0, k_late)]
+    kmask = [copyS(T.mk[:, 0:512], T.OH[:].indirect(T.lu0[:]), klu0, k_wb)]
 
     k = tsV(T.e7[:], T.ei[:], 7.0, A.add)
     k5 = tsV(T.li[:], T.e7[:], 7, A.bitwise_and, k)
@@ -265,7 +266,7 @@ def rank_program(g, core, T, topo):
         G, bank = (T.G0, T.G1)[t % 2], (T.pR0, T.pR1)[t % 2]
         if t > 1:
             wait("v", ksum[t - 2])
-        kg = ttV(G[:], T.win[:].indirect(T.off[:]), T.mk[:, 512 * t:512 * t + 512], A.mult, koff, kmask[t], *kprev)
+        kg = ttV(G[:], T.win[:].indirect(T.off[:]), T.mk[:, 512 * t:512 * t + 512], A.mult, koff, kmask[t], k_late, *kprev)
         if t < 7:
             s = (128 - 16 * (t + 1)) % 128
             mm(bank[:, 0:32], T.WH[:, s:s + 128], T.h16[:, 32 * (t + 1):32 * (t + 2)], True, False, kl8, koff)

@@ -7,9 +7,9 @@ for _n, _w in (("sm", 16), ("rm", 16), ("se", 32), ("rre", 32), ("sx", 4), ("rx"
     SCRATCH[_n] = ("dram", [8, 128, _w], "int32")
 for _n in ("od", "ri"):
     SCRATCH[_n] = ("dram", [8, 128, 8], "float32")
-for _d, _l in (("int32", "W0:1024 A1:1024 cmp:64 ei:256 xi:32 e7:256 li:256 hi:256 e70:32 li0:32 i1:256 pc:1 ci:8 da:256 db:256"),
-               ("float32", "win:5120 W1:1024 W2:1024 adF:1024 OT:64 cf:24"),
-               ("float16", "g1:1024 g2:1024 g3:1024 ad16:1024 gb:1024 c16:64 y16:64 l16:256 h16:256 x16:32 G0:512 G1:512 B9:128 B11:128 C1:128 C2:128 D1:128 D2:128 D3:128 WI:256 WIe:256 WIo:256 WH:256 W1r:256 W3r:256 Wb:256 WT:256 WS:256"),
+for _d, _l in (("int32", "W0:1024 A1:1024 cmp:64 ei:256 xi:32 e7:256 li:256 hi:256 e70:32 li0:32 i1:256 pc:1 ci:8 da:256 db:256 dg:16 dh:16"),
+               ("float32", "win:5120 W1:1024 W2:1024 adF:1024 OT:32 OR:512 cf:24"),
+               ("float16", "g1:1024 g2:1024 g3:1024 ad16:1024 gb:1024 c16:64 y16:64 l16:256 h16:256 x16:32 G0:512 G1:512 B9:128 B11:128 C1:128 C2:128 D1:128 D2:128 D3:128 WI:256 WIe:256 WIo:256 WH:256 W1r:256 W3r:256 Wb:256 WT:256 WS:16 Z8:8"),
                ("uint16", "L1:64 L2:64 L4:64 L8:64 lu0:32 lu:256 off:32")):
     for _e in _l.split():
         SCRATCH[_e.split(":")[0]] = ("sbuf", [128, int(_e.split(":")[1])], _d)
@@ -92,9 +92,9 @@ def rank_program(g, core, T, topo):
     fused(T.sx, T.rx, "ax")
     k_id = done("gi", g.iota(T.win[:, 0:1024], [[1, 1024]], 0, 0, allow_small_or_imprecise_dtypes=True))
 
-    names = ["T", "S", "p", "he", "ho", "r1", "r3", "r9", "r11", "R01", "R03", "uC", "u1", "u2", "u9", "u11", "neg", "k7"]
+    names = ["T", "S", "p", "he", "ho", "r1", "r3", "r9", "r11", "R01", "R03", "uC", "u1", "u2", "u9", "u11", "neg", "k7", "g"]
     col = {n: T.cf[:, i:i + 1] for i, n in enumerate(names)}
-    c15, c7, c16b, cn, cn7 = [T.ci[:, i:i + 1] for i in range(5)]
+    c15, c7, c16b, cn, cn7, cg = [T.ci[:, i:i + 1] for i in range(6)]
     k_a1 = done("v", V.memset(T.A1[:], 0))
     wait("v", k_pc)
     tsV(c15, T.pc[:, 0:1], 15, A.bitwise_and)
@@ -132,12 +132,18 @@ def rank_program(g, core, T, topo):
     k_mat = tsV(T.WI[:], T.db[:], 0.0, A.is_equal)
     I = T.WI[:, 0:128]
     tsV(T.W3r[:], T.db[:], 125.0, A.is_equal, s2=col["r3"], op1=A.mult)
+    tsV(T.Z8[:], T.db[:, 0:8], 0.0, A.is_lt)
+    kg = tsV(cg, T.pc[:, 0:1], 4, A.arith_shift_right)
     k = tsV(cn, c15, -1.0, A.mult, s2=128.0, op1=A.add)
-    copyV(col["k7"], c7)
+    kg = copyV(col["g"], cg, kg)
     k = tsV(cn7, cn, 127, A.bitwise_and, k)
+    kg = tsV(T.dg[:], T.i1[:, 0:16], col["g"], A.subtract, kg)
+    copyV(col["k7"], c7)
     k = copyV(col["neg"], cn7, k)
-    tsV(T.OH[:], T.i1[:, 0:8], col["k7"], A.subtract, s2=128.0, op1=A.is_equal)
-    k_wb = tsV(T.Wb[:], T.db[:], col["neg"], A.is_equal, k)
+    kg = tsV(T.dh[:], T.dg[:], 7, A.bitwise_and, kg)
+    tsV(T.OH[:], T.i1[:, 0:8], col["k7"], A.subtract, k, s2=128.0, op1=A.is_equal)
+    k_wb = tsV(T.Wb[:], T.db[:], col["neg"], A.is_equal)
+    tsV(T.WS[:], T.dh[:], 0.0, A.is_equal, kg, s2=col["S"], op1=A.mult)
 
     nxl, wl = T.rm[:, 0:64, :], T.rm[:, 64:128, :]
     for e in (Y, S):
@@ -157,7 +163,6 @@ def rank_program(g, core, T, topo):
     Y.dma_start(out=T.xi[:], in_=T.rx[:]).then_inc(sem.xl, 16)
     copyS(T.WH[:], T.WI[:], k_mat, scale=128.0)
     copyS(T.WT[:], T.Wb[:], k_wb, scale=col["T"])
-    copyS(T.WS[:], T.Wb[:], scale=col["S"])
     k_late = copyS(T.win[:, 0:1024], T.win[:, 0:1024], k_id, scale=col["T"])
 
     wait("v", ("cl", 16))
@@ -173,17 +178,17 @@ def rank_program(g, core, T, topo):
                 kL = mm(T.pR1[:, 2 * b + h0:64:4], (T.WIe, T.WIo)[h0][:, s:s + 128], T.y16[:, c:c + 16], h == 0, h == 1)
     kL1 = copyV(T.L1[:], T.pR1[:, 0:64], kL)
 
-    def relay(bank, wide, src, shift, n, first, *w):
+    def relay(out, wide, src, shift, first, *w):
         wait("p", *w)
         for r in range(16):
             s = (shift - r) % 128
-            k = mm(bank[:, 0:n], wide[:, s:s + 128], src[:, r::16], first and r == 0, r == 15)
+            k = mm(out, wide[:, s:s + 128], src[:, r::16], first and r == 0, r == 15)
         return k
 
     H = (slice(0, 512), slice(512, 1024))
     wait("v", ("wl", 64))
     kg1 = [ttV(T.g1[:, H[h]], T.W0[:].indirect(T.L1[:, 32 * h:32 * h + 32]), T.A1[:, H[h]], A.add, kL1) for h in range(2)]
-    kr = relay(T.pR0, T.W1r, T.g1, 0, 64, True, k_w1r, *kg1)
+    kr = relay(T.pR0[:, 0:64], T.W1r, T.g1, 0, True, k_w1r, *kg1)
     copyS(T.W1[:, 0:512], T.g1[:, 0:512], kg1[0])
     ks1 = copyS(T.W1[:, 512:768], T.g1[:, 512:768], kg1[1])
     kv1 = copyV(T.W1[:, 768:1024], T.g1[:, 768:1024], kg1[1])
@@ -199,7 +204,7 @@ def rank_program(g, core, T, topo):
     kg2s = copyS(T.g2[:, H[1]], T.W1[:].indirect(T.L2[:, 32:64]), kl, ks1, kv1)
     m0 = mm(pM[0][:], T.C2[:], T.g2[:, H[0]], False, True, kg2v)
     m1 = mm(pM[1][:], T.C2[:], T.g2[:, H[1]], False, True, kg2s)
-    kr = relay(T.pR1, T.W1r, T.g2, 0, 64, True, kL1)
+    kr = relay(T.pR1[:, 0:64], T.W1r, T.g2, 0, True, kL1)
     kw2v = copyV(T.W2[:, H[0]], pM[0][:], m0)
     kw2s = copyS(T.W2[:, H[1]], pM[1][:], m1)
     kl = copyV(T.L4[:], T.pR1[:, 0:64], kr)
@@ -212,7 +217,7 @@ def rank_program(g, core, T, topo):
     kg3s = copyS(T.g3[:, H[1]], T.W2[:].indirect(T.L4[:, 32:64]), kl, kw2v, kw2s)
     m0 = mm(pN[0][:], T.D3[:], T.g3[:, H[0]], False, True, kg3v)
     m1 = mm(pN[1][:], T.D3[:], T.g3[:, H[1]], False, True, kg3s)
-    kr = relay(T.pR0, T.W3r, T.g3, 0, 64, True, kl, k_wb)
+    kr = relay(T.pR0[:, 0:64], T.W3r, T.g3, 0, True, kl, k_wb)
     kad = []
     for h in range(2):
         mm(pA[h][:], T.B9[:], T.g2[:, H[h]], False, False)
@@ -242,7 +247,7 @@ def rank_program(g, core, T, topo):
     mm(T.pR1[:, 0:32], I, T.x16[:], True, False, kl)
     ko = mm(T.pR1[:, 0:32], T.WH[:, 0:128], T.h16[:, 0:32], False, True)
     klu = copyV(T.lu[:], T.pM1[:, 0:256], kt)
-    koff = copyV(T.off[:], T.pR1[:, 0:32], ko)
+    koff0 = copyV(T.off[:], T.pR1[:, 0:32], ko)
 
     nS = 1024 - VC
     kprev = [kb1v, kb1s]
@@ -261,33 +266,46 @@ def rank_program(g, core, T, topo):
     for t in range(1, 8):
         kmask.append(copyS(T.mk[:, 512 * t:512 * t + 512], T.OH[:].indirect(T.lu[:, 32 * t:32 * t + 32]), klu))
 
-    ksum = {}
-    for t in range(8):
-        G, bank = (T.G0, T.G1)[t % 2], (T.pR0, T.pR1)[t % 2]
+    for z in range(2):
+        mm(pM[z][0:8, 0:256], T.Z8[:], T.g3[:, 0:256], True, False, kw2v, klu)
+    Gs, pR = (T.G0, T.G1), (T.pR0, T.pR1)
+    ksum, kgat = {}, {}
+    koff = [koff0, koff0]
+
+    def gather(t, z):
         if t > 1:
             wait("v", ksum[t - 2])
-        kg = ttV(G[:], T.win[:].indirect(T.off[:]), T.mk[:, 512 * t:512 * t + 512], A.mult, koff, kmask[t], k_late, *kprev)
-        if t < 7:
-            s = (128 - 16 * (t + 1)) % 128
-            mm(bank[:, 0:32], T.WH[:, s:s + 128], T.h16[:, 32 * (t + 1):32 * (t + 2)], True, False, kl8, koff)
-        kr = relay(bank, T.WT, G, 112, 32, t == 7, kg, koff)
-        if t < 7:
-            koff = copyV(T.off[:], bank[:, 0:32], kr)
-        else:
-            klast = copyV(T.OT[:, 0:32], bank[:, 0:32], kr)
+        c = slice(256 * z, 256 * z + 256)
+        m = T.mk[:, 512 * t + 256 * z:512 * t + 256 * z + 256]
+        kgat[t, z] = ttV(Gs[t % 2][:, c], T.win[:].indirect(T.off[:, 16 * z:16 * z + 16]), m, A.mult, koff[z], kmask[t], k_late, *kprev)
+    gather(0, 0)
+    gather(0, 1)
+    for t in range(8):
+        G = Gs[t % 2]
+        for z in range(2):
+            o = pR[z][:, 0:16]
+            if t < 7:
+                s, c = (128 - 16 * (t + 1)) % 128, 32 * (t + 1) + 16 * z
+                mm(o, T.WH[:, s:s + 128], T.h16[:, c:c + 16], True, False, kl8, koff0, koff[z])
+            kr = relay(o, T.WT, G[:, 256 * z:256 * z + 256], 112, t == 7, kgat[t, z], koff[z])
+            dst = T.off if t < 7 else T.OT
+            koff[z] = copyV(dst[:, 16 * z:16 * z + 16], o, kr)
+            if t < 7:
+                gather(t + 1, z)
         for r in range(16):
-            s = (16 * t - r) % 128
-            wait("p", kw2v)
-            ins = P.matmul(out=T.pM0[:, 0:32], lhsT=T.WS[:, s:s + 128], rhs=G[:, r::16], start=(t == 0 and r == 0), stop=(t == 7 and r == 15))
-        ksum[t] = done("p", ins)
-    ktot = copyS(T.OT[:, 32:64], T.pM0[:, 0:32], ksum[7])
+            last = t == 7 and r % 8 == 7
+            ins = P.matmul(out=pM[r // 8][0:8, 32 * (r % 8):32 * (r % 8) + 32], lhsT=T.WS[:, t:t + 8], rhs=G[:, r::16], start=False, stop=last)
+            if last or r == 15:
+                ksum[t, r] = ksum[t] = done("p", ins)
+    ktv = copyV(T.OR[0:8, 0:256], pM[0][0:8, 0:256], ksum[7, 7])
+    kts = copyS(T.OR[0:8, 256:512], pM[1][0:8, 0:256], ksum[7, 15])
 
-    wait("y", klast)
-    Y.dma_start(out=T.od[:, 0:64, :], in_=T.OT[:, 0:32]).then_inc(sem.st, 16)
-    Y.dma_start(out=T.ri[me, 0:64, :], in_=T.OT[mine, 0:32]).then_inc(sem.own3, 16)
-    wait("s", ktot)
-    S.dma_start(out=T.od[:, 64:128, :], in_=T.OT[:, 32:64]).then_inc(sem.st, 16)
-    S.dma_start(out=T.ri[me, 64:128, :], in_=T.OT[mine, 32:64]).then_inc(sem.own3, 16)
+    wait("y", *koff)
+    Y.dma_start(out=T.od[:, 0:64, :], in_=T.OT[:]).then_inc(sem.st, 16)
+    Y.dma_start(out=T.ri[me, 0:64, :], in_=T.OT[mine, :]).then_inc(sem.own3, 16)
+    wait("s", ktv, kts)
+    S.dma_start(out=T.od[:, 64:128, :], in_=T.OR[0:8, :]).then_inc(sem.st, 16)
+    S.dma_start(out=T.ri[me, 64:128, :], in_=T.OR[me:me + 1, :]).then_inc(sem.own3, 16)
     g.wait_ge(sem.st, 32)
     fused(T.od, T.ri, "ar")
     for e in (Y, S):

@@ -1,21 +1,23 @@
 from concourse.bass import DstId, RemoteDMATransfer
 from concourse.mybir import AluOpType, ActivationFunctionType
 
+VA = 576
 VC = 704
-SCRATCH = {"OH": ("sbuf", [128, 8], "float32"), "mk": ("sbuf", [128, 4096], "bfloat16")}
+BIAS = 1024.0 * 1024.0
+SCRATCH = {"OH": ("sbuf", [128, 32], "float32"), "mk": ("sbuf", [128, 4096], "bfloat16")}
 for _n, _w in (("sm", 16), ("rm", 16), ("se", 32), ("rre", 32), ("sx", 4), ("rx", 4)):
     SCRATCH[_n] = ("dram", [8, 128, _w], "int32")
 for _n in ("od", "ri"):
     SCRATCH[_n] = ("dram", [8, 128, 8], "float32")
-for _d, _l in (("int32", "W0:1024 A1:1024 cmp:64 ei:256 xi:32 e7:256 li:256 hi:256 e70:32 li0:32 i1:256 pc:1 ci:8 da:256 db:256 dg:16 dh:16"),
+for _d, _l in (("int32", "W0:1024 A1:1024 cmp:64 ei:256 xi:32 i1:264 pc:1 ci:8 da:264 db:264 dg:16 dh:16 dq:32 dr:32"),
                ("float32", "win:5120 W1:1024 W2:1024 adF:1024 OT:32 OR:512 cf:24"),
-               ("float16", "g1:1024 g2:1024 g3:1024 ad16:1024 gb:1024 c16:64 y16:64 l16:256 h16:256 x16:32 G0:512 G1:512 B9:128 B11:128 C1:128 C2:128 D1:128 D2:128 D3:128 WI:256 WIe:256 WIo:256 WH:256 W1r:256 W3r:256 Wb:256 WT:256 WS:16 Z8:8"),
+               ("float16", "g1:1024 g2:1024 g3:1024 a16:448 ad16:1024 gb:1024 c16:64 y16:64 e16:256 h16:256 x16:32 G0:512 G1:512 B9:128 B11:128 D1:128 D2:128 D3:128 WI:264 WIe:256 WIo:256 WH:256 W1r:256 W3r:256 Wb:256 WT:256 WS:16 Z8:8"),
                ("uint16", "L1:64 L2:64 L4:64 L8:64 lu0:32 lu:256 off:32")):
     for _e in _l.split():
         SCRATCH[_e.split(":")[0]] = ("sbuf", [128, int(_e.split(":")[1])], _d)
 for _n in ("pR0", "pR1", "pM0", "pM1", "pN0", "pN1", "pA0", "pA1"):
     SCRATCH[_n] = ("psum", [128, 512], "float32")
-SEMAPHORES = ["ld", "own", "ld2", "own2", "am", "ae", "ax", "cl", "wl", "xl", "v", "s", "p", "gi", "ls", "st", "own3", "ar", "fin"]
+SEMAPHORES = ["ld", "own", "ld2", "own2", "am", "ae", "ax", "cl", "wl", "el", "xl", "v", "s", "p", "gi", "ls", "st", "own3", "ar", "fin"]
 
 
 def rank_program(g, core, T, topo):
@@ -84,7 +86,7 @@ def rank_program(g, core, T, topo):
         q.dma_start(out=out, in_=in_).then_inc(sem[name], 16)
 
     k_pc = done("gi", g.iota(T.pc[:, 0:1], [[0, 1]], 0, 1))
-    k_i1 = done("gi", g.iota(T.i1[:], [[1, 256]], 128, 0))
+    k_i1 = done("gi", g.iota(T.i1[:], [[1, 264]], 128, 0))
     g.wait_ge(sem.ld, 32)
     fused(T.sm, T.rm, "am")
     g.wait_ge(sem.ld2, 32)
@@ -92,7 +94,7 @@ def rank_program(g, core, T, topo):
     fused(T.sx, T.rx, "ax")
     k_id = done("gi", g.iota(T.win[:, 0:1024], [[1, 1024]], 0, 0, allow_small_or_imprecise_dtypes=True))
 
-    names = ["T", "S", "p", "he", "ho", "r1", "r3", "r9", "r11", "R01", "R03", "uC", "u1", "u2", "u9", "u11", "neg", "k7", "g"]
+    names = ["T", "S", "p", "he", "ho", "r1", "r3", "r9", "r11", "R01", "R03", "u1", "u2", "u9", "u11", "neg", "k7", "g"]
     col = {n: T.cf[:, i:i + 1] for i, n in enumerate(names)}
     c15, c7, c16b, cn, cn7, cg = [T.ci[:, i:i + 1] for i in range(6)]
     k_a1 = done("v", V.memset(T.A1[:], 0))
@@ -104,46 +106,48 @@ def rank_program(g, core, T, topo):
     kT = tsV(col["T"], c15, 8.0, A.is_lt, kc)
     tsV(col["he"], c16b, 0.0, A.is_equal)
     tsV(col["ho"], c16b, 16.0, A.is_equal)
-    kr1 = tsV(col["r1"], c15, 1.0, A.is_equal)
+    tsV(col["r1"], c15, 1.0, A.is_equal)
+    tsV(col["r3"], c15, 3.0, A.is_equal)
     k = tsV(T.da[:], T.i1[:], col["p"], A.subtract, k_i1, kp)
     k_db = tsV(T.db[:], T.da[:], 127, A.bitwise_and, k)
     for i in range(4):
-        k_w0 = tsV(T.W0[:, 256 * i:256 * i + 256], T.i1[:], float(256 * i - 128), A.add, kT, s2=col["T"], op1=A.mult)
-    tsV(T.WIe[:], T.db[:], 0.0, A.is_equal, k_db, kr1, s2=col["he"], op1=A.mult)
-    k_wio = tsV(T.WIo[:], T.db[:], 0.0, A.is_equal, s2=col["ho"], op1=A.mult)
-    k_w1r = tsV(T.W1r[:], T.db[:], 127.0, A.is_equal, s2=col["r1"], op1=A.mult)
+        k_w0 = tsV(T.W0[:, 256 * i:256 * i + 256], T.i1[:, 0:256], float(256 * i - 128), A.add, kT, s2=col["T"], op1=A.mult)
+    k_mat = tsV(T.WI[:], T.db[:], 0.0, A.is_equal, k_db)
+    I = T.WI[:, 0:128]
     tsV(col["R01"], c7, 2.0, A.is_lt)
     tsV(col["R03"], c7, 4.0, A.is_lt)
     tsV(col["r11"], c15, 11.0, A.is_equal)
-    tsV(col["r3"], c15, 3.0, A.is_equal)
     tsV(col["S"], c15, 8.0, A.is_ge)
     k = tsV(col["r9"], c15, 9.0, A.is_equal)
-    for n, f in (("uC", 2.0), ("u1", 6.0), ("u2", 4.0)):
+    for n, f in (("u1", 6.0), ("u2", 4.0)):
         tsV(col[n], col["r9"], f, A.mult, k, s2=col["R01"], op1=A.add)
     tsV(col["u9"], col["r9"], 8.0, A.mult)
     k = tsV(col["u11"], col["r11"], 8.0, A.mult)
-    tsV(T.C1[:], T.db[:, 0:128], col["uC"], A.is_lt, k)
-    tsV(T.C2[:], T.db[:, 0:128], 2.0, A.is_equal, s2=col["R01"], op1=A.mult)
-    tsV(T.D1[:], T.db[:, 0:128], col["u1"], A.is_lt)
+    tsV(T.D1[:], T.db[:, 0:128], col["u1"], A.is_lt, k)
     tsV(T.D2[:], T.db[:, 126:254], col["u2"], A.is_lt)
     tsV(T.D3[:], T.db[:, 0:128], 4.0, A.is_equal, s2=col["R03"], op1=A.mult)
     tsV(T.B9[:], T.db[:, 1:129], col["u9"], A.is_lt)
     tsV(T.B11[:], T.db[:, 3:131], col["u11"], A.is_lt)
-    k_mat = tsV(T.WI[:], T.db[:], 0.0, A.is_equal)
-    I = T.WI[:, 0:128]
-    tsV(T.W3r[:], T.db[:], 125.0, A.is_equal, s2=col["r3"], op1=A.mult)
     tsV(T.Z8[:], T.db[:, 0:8], 0.0, A.is_lt)
     kg = tsV(cg, T.pc[:, 0:1], 4, A.arith_shift_right)
     k = tsV(cn, c15, -1.0, A.mult, s2=128.0, op1=A.add)
+    kk = copyV(col["k7"], c7)
     kg = copyV(col["g"], cg, kg)
     k = tsV(cn7, cn, 127, A.bitwise_and, k)
+    kk = tsV(T.dq[:], T.i1[:, 0:32], col["k7"], A.subtract, kk)
     kg = tsV(T.dg[:], T.i1[:, 0:16], col["g"], A.subtract, kg)
-    copyV(col["k7"], c7)
     k = copyV(col["neg"], cn7, k)
+    kk = tsV(T.dr[:], T.dq[:], 7, A.bitwise_and, kk)
     kg = tsV(T.dh[:], T.dg[:], 7, A.bitwise_and, kg)
-    tsV(T.OH[:], T.i1[:, 0:8], col["k7"], A.subtract, k, s2=128.0, op1=A.is_equal)
-    k_wb = tsV(T.Wb[:], T.db[:], col["neg"], A.is_equal)
-    tsV(T.WS[:], T.dh[:], 0.0, A.is_equal, kg, s2=col["S"], op1=A.mult)
+    k_wb = tsV(T.Wb[:], T.db[:, 0:256], col["neg"], A.is_equal, k)
+    k_oh = tsV(T.OH[:], T.dr[:], 1.0, A.is_equal, kk)
+    k_ws = tsV(T.WS[:], T.dh[:], 0.0, A.is_equal, kg, s2=col["S"], op1=A.mult)
+
+    copyS(T.WIe[:], T.WI[:, 0:256], k_mat, scale=col["he"])
+    k_wio = copyS(T.WIo[:], T.WI[:, 0:256], scale=col["ho"])
+    k_w1r = copyS(T.W1r[:, 0:255], T.WI[:, 1:256], scale=col["r1"])
+    k_w3r = copyS(T.W3r[:, 0:255], T.WI[:, 3:258], scale=col["r3"])
+    k_wh = copyS(T.WH[:], T.WI[:, 0:256], scale=1024.0)
 
     nxl, wl = T.rm[:, 0:64, :], T.rm[:, 64:128, :]
     for e in (Y, S):
@@ -158,12 +162,11 @@ def rank_program(g, core, T, topo):
     Y.dma_start(out=T.A1[8::16, :], in_=wl).then_inc(sem.wl, 16)
     Y.wait_ge(sem.own2, 32)
     Y.wait_ge(sem.ae, N - 1)
-    Y.dma_start(out=T.ei[:], in_=T.rre[:]).then_inc(sem.xl, 16)
+    Y.dma_start(out=T.ei[:], in_=T.rre[:]).then_inc(sem.el, 16)
     Y.wait_ge(sem.ax, N - 1)
     Y.dma_start(out=T.xi[:], in_=T.rx[:]).then_inc(sem.xl, 16)
-    copyS(T.WH[:], T.WI[:], k_mat, scale=128.0)
-    copyS(T.WT[:], T.Wb[:], k_wb, scale=col["T"])
     k_late = copyS(T.win[:, 0:1024], T.win[:, 0:1024], k_id, scale=col["T"])
+    k_wt = copyS(T.WT[:], T.Wb[:], k_wb, scale=col["T"])
 
     wait("v", ("cl", 16))
     k = copyV(T.c16[:], T.cmp[:])
@@ -176,6 +179,9 @@ def rank_program(g, core, T, topo):
                 s = 0 if h == h0 else (112 if h == 1 else 16)
                 c = 32 * b + 16 * h
                 kL = mm(T.pR1[:, 2 * b + h0:64:4], (T.WIe, T.WIo)[h0][:, s:s + 128], T.y16[:, c:c + 16], h == 0, h == 1)
+    wait("s", ("wl", 64))
+    k_a16 = copyS(T.a16[:], T.A1[:, VA:1024])
+    wait("v", ("wl", 64))
     kL1 = copyV(T.L1[:], T.pR1[:, 0:64], kL)
 
     def relay(out, wide, src, shift, first, *w):
@@ -185,127 +191,137 @@ def rank_program(g, core, T, topo):
             k = mm(out, wide[:, s:s + 128], src[:, r::16], first and r == 0, r == 15)
         return k
 
+    pN, pA = (T.pN0, T.pN1), (T.pA0, T.pA1)
     H = (slice(0, 512), slice(512, 1024))
-    wait("v", ("wl", 64))
-    kg1 = [ttV(T.g1[:, H[h]], T.W0[:].indirect(T.L1[:, 32 * h:32 * h + 32]), T.A1[:, H[h]], A.add, kL1) for h in range(2)]
-    kr = relay(T.pR0[:, 0:64], T.W1r, T.g1, 0, True, k_w1r, *kg1)
-    copyS(T.W1[:, 0:512], T.g1[:, 0:512], kg1[0])
-    ks1 = copyS(T.W1[:, 512:768], T.g1[:, 512:768], kg1[1])
-    kv1 = copyV(T.W1[:, 768:1024], T.g1[:, 768:1024], kg1[1])
+    nA = 1024 - VA
+    kg1v = ttV(T.g1[:, 0:VA], T.W0[:].indirect(T.L1[:, 0:VA // 16]), T.A1[:, 0:VA], A.add, kL1)
+    kg1s = copyS(T.g1[:, VA:1024], T.W0[:].indirect(T.L1[:, VA // 16:64]), kL1)
+    mm(T.pM0[:, 0:nA], I, T.a16[:], True, False, k_a16)
+    ka = mm(T.pM0[:, 0:nA], I, T.g1[:, VA:1024], False, True, kg1s)
+    kr = relay(T.pR0[:, 0:64], T.W1r, T.g1, 0, True, k_w1r, kg1v)
+    ks1 = copyS(T.W1[:, VA:1024], T.pM0[:, 0:nA], ka)
+    kv1 = copyV(T.W1[:, 0:VA], T.g1[:, 0:VA], kg1v)
+    wait("v", ("el", 16))
+    klu0 = copyV(T.lu0[:], T.ei[:, 0:32])
     kl = copyV(T.L2[:], T.pR0[:, 0:64], kr)
 
-    pM, pN, pA = (T.pM0, T.pM1), (T.pN0, T.pN1), (T.pA0, T.pA1)
-    wait("p", k_mat)
-    for h in range(2):
-        mm(pM[h][:], T.C1[:], T.g1[:, H[h]], True, False)
-    for h in range(2):
-        mm(pN[h][:], T.D1[:], T.g1[:, H[h]], True, False)
+    mm(pN[0][:], T.D1[:], T.g1[:, H[0]], True, False)
+    mm(pN[1][:], T.D1[:], T.g1[:, H[1]], True, False)
+    mm(pN[1][:, VA - 512:512], T.D1[:], T.a16[:], False, False)
+    mm(pA[0][:], T.B9[:], T.g1[:, H[0]], True, False)
     kg2v = copyV(T.g2[:, H[0]], T.W1[:].indirect(T.L2[:, 0:32]), kl, ks1, kv1)
     kg2s = copyS(T.g2[:, H[1]], T.W1[:].indirect(T.L2[:, 32:64]), kl, ks1, kv1)
-    m0 = mm(pM[0][:], T.C2[:], T.g2[:, H[0]], False, True, kg2v)
-    m1 = mm(pM[1][:], T.C2[:], T.g2[:, H[1]], False, True, kg2s)
+    m0 = mm(pN[0][:], T.D2[:], T.g2[:, H[0]], False, True, kg2v)
+    m1 = mm(pN[1][:], T.D2[:], T.g2[:, H[1]], False, True, kg2s)
     kr = relay(T.pR1[:, 0:64], T.W1r, T.g2, 0, True, kL1)
-    kw2v = copyV(T.W2[:, H[0]], pM[0][:], m0)
-    kw2s = copyS(T.W2[:, H[1]], pM[1][:], m1)
+    k_e16 = copyV(T.e16[:], T.ei[:])
+    kmask = {(0, 0): copyS(T.mk[:, 0:256], T.OH[:].indirect(T.lu0[:, 0:16]), klu0, k_oh)}
+    kw2v = copyV(T.W2[:, H[0]], pN[0][:], m0)
+    kw2s = copyS(T.W2[:, H[1]], pN[1][:], m1)
     kl = copyV(T.L4[:], T.pR1[:, 0:64], kr)
 
-    for h in range(2):
-        mm(pN[h][:], T.D2[:], T.g2[:, H[h]], False, False)
-    for h in range(2):
-        mm(pA[h][:], T.B9[:], T.g1[:, H[h]], True, False)
-    kg3v = copyV(T.g3[:, H[0]], T.W2[:].indirect(T.L4[:, 0:32]), kl, kw2v, kw2s)
-    kg3s = copyS(T.g3[:, H[1]], T.W2[:].indirect(T.L4[:, 32:64]), kl, kw2v, kw2s)
-    m0 = mm(pN[0][:], T.D3[:], T.g3[:, H[0]], False, True, kg3v)
-    m1 = mm(pN[1][:], T.D3[:], T.g3[:, H[1]], False, True, kg3s)
-    kr = relay(T.pR0[:, 0:64], T.W3r, T.g3, 0, True, kl, k_wb)
-    kad = []
+    mm(pA[1][:], T.B9[:], T.g1[:, H[1]], True, False)
+    mm(pA[1][:, VA - 512:512], T.B9[:], T.a16[:], False, False)
     for h in range(2):
         mm(pA[h][:], T.B9[:], T.g2[:, H[h]], False, False)
+    kg3v = copyV(T.g3[:, H[0]], T.W2[:].indirect(T.L4[:, 0:32]), kl, kw2v, kw2s)
+    kg3s = copyS(T.g3[:, H[1]], T.W2[:].indirect(T.L4[:, 32:64]), kl, kw2v, kw2s)
+    m3, kad = [], []
+    for h in range(2):
+        m3.append(mm(pN[h][:], T.D3[:], T.g3[:, H[h]], True, True, (kg3v, kg3s)[h]))
         kad.append(mm(pA[h][:], T.B11[:], T.g3[:, H[h]], False, True))
-    kb1v = copyV(T.win[:, 1024:1536], pN[0][:], m0)
-    kb1s = copyS(T.win[:, 1536:2048], pN[1][:], m1)
-    wait("v", ("xl", 32))
-    k = tsV(T.e70[:], T.ei[:, 0:32], 7.0, A.add)
-    k = tsV(T.li0[:], T.e70[:], 7, A.bitwise_and, k)
-    klu0 = copyV(T.lu0[:], T.li0[:], k)
-    kl8 = copyV(T.L8[:], T.pR0[:, 0:64], kr)
-    kmask = [copyS(T.mk[:, 0:512], T.OH[:].indirect(T.lu0[:]), klu0, k_wb)]
-
-    k = tsV(T.e7[:], T.ei[:], 7.0, A.add)
-    k5 = tsV(T.li[:], T.e7[:], 7, A.bitwise_and, k)
-    k6 = tsV(T.hi[:], T.e7[:], 56, A.bitwise_and)
-    k5 = copyV(T.l16[:], T.li[:], k5)
-    k6 = copyV(T.h16[:], T.hi[:], k6)
-    k7 = copyV(T.x16[:], T.xi[:])
-    kadV = copyV(T.adF[:, 0:512], pA[0][:], kad[0])
+    kr = relay(T.pR0[:, 0:64], T.W3r, T.g3, 0, True, k_w3r, kl)
+    k_h16 = tsV(T.h16[:], T.ei[:], 0.125, A.mult, s2=1024.4375, op1=A.add)
+    kmask[0, 1] = copyS(T.mk[:, 256:512], T.OH[:].indirect(T.lu0[:, 16:32]))
+    ttV(T.win[:, 1024:1536], T.W2[:, H[0]], pN[0][:], A.add, m3[0])
+    kb1 = ttV(T.win[:, 1536:2048], T.W2[:, H[1]], pN[1][:], A.add, m3[1])
+    copyS(T.adF[:, 0:512], pA[0][:], kad[0])
     kadS = copyS(T.adF[:, 512:VC], pA[1][:, 0:VC - 512], kad[1])
     kadT = copyS(T.ad16[:, VC:1024], pA[1][:, VC - 512:512], kad[1])
-    wait("p", k5, k6, k7, k_late)
-    for t in range(8):
+    kl8 = copyV(T.L8[:], T.pR0[:, 0:64], kr)
+    for t in range(1, 8):
         s = (128 - 16 * t) % 128
-        kt = mm(T.pM1[:, 32 * t:32 * t + 32], T.WI[:, s:s + 128], T.l16[:, 32 * t:32 * t + 32], True, True, kw2s)
-    mm(T.pR1[:, 0:32], I, T.x16[:], True, False, kl)
-    ko = mm(T.pR1[:, 0:32], T.WH[:, 0:128], T.h16[:, 0:32], False, True)
-    klu = copyV(T.lu[:], T.pM1[:, 0:256], kt)
-    koff0 = copyV(T.off[:], T.pR1[:, 0:32], ko)
+        kt = mm(T.pM1[:, 32 * t:32 * t + 32], T.WI[:, s:s + 128], T.e16[:, 32 * t:32 * t + 32], True, True, k_e16)
 
     nS = 1024 - VC
-    kprev = [kb1v, kb1s]
-    kps = [kb1v, kb1s]
+    kprev = [kb1]
+    kps = [kb1]
     for B in range(2, 5):
         a = 1024 * (B - 1)
         src = T.win[:, a:a + 1024]
         bank = pN[B % 2]
-        kv = ttV(T.win[:, a + 1024:a + 1024 + VC], src.indirect(T.L8[:, 0:VC // 16]), T.adF[:, 0:VC], A.add, kl8, kadS, kadV, *kprev)
+        kv = ttV(T.win[:, a + 1024:a + 1024 + VC], src.indirect(T.L8[:, 0:VC // 16]), T.adF[:, 0:VC], A.add, kl8, kadS, *kprev)
         kg = copyS(T.gb[:, VC:1024], src.indirect(T.L8[:, VC // 16:64]), kl8, kadT, *kprev)
         mm(bank[:, 0:nS], I, T.ad16[:, VC:1024], True, False, kadT, *kps)
         km = mm(bank[:, 0:nS], I, T.gb[:, VC:1024], False, True, kg)
         ks = copyS(T.win[:, a + 1024 + VC:a + 2048], bank[:, 0:nS], km)
         kprev = [kv, ks]
         kps = [ks]
-    for t in range(1, 8):
-        kmask.append(copyS(T.mk[:, 512 * t:512 * t + 512], T.OH[:].indirect(T.lu[:, 32 * t:32 * t + 32]), klu))
+        if B == 2:
+            wait("v", ("xl", 16))
+            kx = copyV(T.x16[:], T.xi[:])
+            mm(T.pR1[:, 0:32], I, T.x16[:], True, False, kx, kl)
+            ko = mm(T.pR1[:, 0:32], T.WH[:, 0:128], T.h16[:, 0:32], False, True, k_h16, k_wh)
+            klu1 = copyV(T.lu[:, 32:64], T.pM1[:, 32:64], kt)
+        if B == 3:
+            koff0 = tsV(T.off[:], T.pR1[:, 0:32], -BIAS, A.add, ko)
 
     for z in range(2):
-        mm(pM[z][0:8, 0:256], T.Z8[:], T.g3[:, 0:256], True, False, kw2v, klu)
+        mm(pA[z][0:8, 0:256], T.Z8[:], T.g3[:, 0:256], True, False, kadT)
     Gs, pR = (T.G0, T.G1), (T.pR0, T.pR1)
     ksum, kgat = {}, {}
     koff = [koff0, koff0]
+
+    def mask(t, k):
+        kmask[t, 0] = kmask[t, 1] = copyS(T.mk[:, 512 * t:512 * t + 512], T.OH[:].indirect(T.lu[:, 32 * t:32 * t + 32]), k)
 
     def gather(t, z):
         if t > 1:
             wait("v", ksum[t - 2])
         c = slice(256 * z, 256 * z + 256)
         m = T.mk[:, 512 * t + 256 * z:512 * t + 256 * z + 256]
-        kgat[t, z] = ttV(Gs[t % 2][:, c], T.win[:].indirect(T.off[:, 16 * z:16 * z + 16]), m, A.mult, koff[z], kmask[t], k_late, *kprev)
+        kgat[t, z] = ttV(Gs[t % 2][:, c], T.win[:].indirect(T.off[:, 16 * z:16 * z + 16]), m, A.mult, koff[z], kmask[t, z], k_late, *kprev)
+
+    def weights(t):
+        for r in range(16):
+            last = t == 7 and r % 8 == 7
+            ins = P.matmul(out=pA[r // 8][0:8, 32 * (r % 8):32 * (r % 8) + 32], lhsT=T.WS[:, t:t + 8], rhs=Gs[t % 2][:, r::16], start=False, stop=last)
+            if last or r == 15:
+                ksum[t, r] = ksum[t] = done("p", ins)
+
+    mask(1, klu1)
     gather(0, 0)
     gather(0, 1)
+    klu = copyV(T.lu[:, 64:256], T.pM1[:, 64:256])
+    for t in range(2, 8):
+        mask(t, klu)
+    wait("p", k_wt, k_ws)
     for t in range(8):
-        G = Gs[t % 2]
         for z in range(2):
             o = pR[z][:, 0:16]
             if t < 7:
                 s, c = (128 - 16 * (t + 1)) % 128, 32 * (t + 1) + 16 * z
                 mm(o, T.WH[:, s:s + 128], T.h16[:, c:c + 16], True, False, kl8, koff0, koff[z])
-            kr = relay(o, T.WT, G[:, 256 * z:256 * z + 256], 112, t == 7, kgat[t, z], koff[z])
-            dst = T.off if t < 7 else T.OT
-            koff[z] = copyV(dst[:, 16 * z:16 * z + 16], o, kr)
+            elif z == 1:
+                wait("p", kgat[7, 1])
+                weights(7)
+                ktv = copyV(T.OR[0:8, 0:256], pA[0][0:8, 0:256], ksum[7, 7])
+                kts = copyS(T.OR[0:8, 256:512], pA[1][0:8, 0:256], ksum[7, 15])
+            kr = relay(o, T.WT, Gs[t % 2][:, 256 * z:256 * z + 256], 112, t == 7, kgat[t, z], koff[z])
             if t < 7:
+                koff[z] = tsV(T.off[:, 16 * z:16 * z + 16], o, -BIAS, A.add, kr)
                 gather(t + 1, z)
-        for r in range(16):
-            last = t == 7 and r % 8 == 7
-            ins = P.matmul(out=pM[r // 8][0:8, 32 * (r % 8):32 * (r % 8) + 32], lhsT=T.WS[:, t:t + 8], rhs=G[:, r::16], start=False, stop=last)
-            if last or r == 15:
-                ksum[t, r] = ksum[t] = done("p", ins)
-    ktv = copyV(T.OR[0:8, 0:256], pM[0][0:8, 0:256], ksum[7, 7])
-    kts = copyS(T.OR[0:8, 256:512], pM[1][0:8, 0:256], ksum[7, 15])
+            else:
+                koff[z] = copyV(T.OT[:, 16 * z:16 * z + 16], o, kr)
+        if t < 7:
+            weights(t)
 
-    wait("y", *koff)
-    Y.dma_start(out=T.od[:, 0:64, :], in_=T.OT[:]).then_inc(sem.st, 16)
-    Y.dma_start(out=T.ri[me, 0:64, :], in_=T.OT[mine, :]).then_inc(sem.own3, 16)
     wait("s", ktv, kts)
     S.dma_start(out=T.od[:, 64:128, :], in_=T.OR[0:8, :]).then_inc(sem.st, 16)
     S.dma_start(out=T.ri[me, 64:128, :], in_=T.OR[me:me + 1, :]).then_inc(sem.own3, 16)
+    wait("y", *koff)
+    Y.dma_start(out=T.od[:, 0:64, :], in_=T.OT[:]).then_inc(sem.st, 16)
+    Y.dma_start(out=T.ri[me, 0:64, :], in_=T.OT[mine, :]).then_inc(sem.own3, 16)
     g.wait_ge(sem.st, 32)
     fused(T.od, T.ri, "ar")
     for e in (Y, S):

@@ -2,22 +2,23 @@ from concourse.bass import DstId, RemoteDMATransfer
 from concourse.mybir import AluOpType, ActivationFunctionType
 
 VA = 576
-VC = 704
-BIAS = 1024.0 * 1024.0
+VC = 736
+VB = 896
+MAGIC = 1.5 * 2.0 ** 23
 SCRATCH = {"OH": ("sbuf", [128, 32], "float32"), "mk": ("sbuf", [128, 4096], "bfloat16")}
 for _n, _w in (("sm", 16), ("rm", 16), ("se", 32), ("rre", 32), ("sx", 4), ("rx", 4)):
     SCRATCH[_n] = ("dram", [8, 128, _w], "int32")
 for _n in ("od", "ri"):
     SCRATCH[_n] = ("dram", [8, 128, 8], "float32")
-for _d, _l in (("int32", "W0:1024 A1:1024 cmp:64 ei:256 xi:32 i1:264 pc:1 ci:8 da:264 db:264 dg:16 dh:16 dq:32 dr:32"),
-               ("float32", "win:5120 W1:1024 W2:1024 adF:1024 OT:32 OR:512 cf:24"),
-               ("float16", "g1:1024 g2:1024 g3:1024 a16:448 ad16:1024 gb:1024 c16:64 y16:64 e16:256 h16:256 x16:32 G0:512 G1:512 B9:128 B11:128 D1:128 D2:128 D3:128 WI:264 WIe:256 WIo:256 WH:256 W1r:256 W3r:256 Wb:256 WT:256 WS:16 Z8:8"),
+for _d, _l in (("int32", "W0:1024 A1:1024 cmp:64 ei:256 xi:32 pc:1 ci:8 da:264 db:264 dr:32"),
+               ("float32", "win:5120 W1:1024 W2:1024 adF:1024 OL:32 OD:32 OT:32 cf:24 R1:224 R2:224"),
+               ("float16", "g1:1024 g2:1024 g3:1024 a16:512 gb:1024 c16:64 y16:64 e16:256 h16:256 x16:32 G0:512 G1:512 K1:128 E1:128 E2:128 B15:128 WI:264 WIe:256 WIo:256 WH:256 W7r:256 WT:256 WT7:256 cst:32 w0:80 w1:80 v0:32 v1:32"),
                ("uint16", "L1:64 L2:64 L4:64 L8:64 lu0:32 lu:256 off:32")):
     for _e in _l.split():
         SCRATCH[_e.split(":")[0]] = ("sbuf", [128, int(_e.split(":")[1])], _d)
 for _n in ("pR0", "pR1", "pM0", "pM1", "pN0", "pN1", "pA0", "pA1"):
     SCRATCH[_n] = ("psum", [128, 512], "float32")
-SEMAPHORES = ["ld", "own", "ld2", "own2", "am", "ae", "ax", "cl", "wl", "el", "xl", "v", "s", "p", "gi", "ls", "st", "own3", "ar", "fin"]
+SEMAPHORES = ["ld", "own", "ld2", "own2", "am", "ae", "ax", "cl", "wl", "al", "el", "xl", "v", "s", "p", "gi", "ls", "st", "own3", "ar", "fin"]
 
 
 def rank_program(g, core, T, topo):
@@ -59,9 +60,9 @@ def rank_program(g, core, T, topo):
         wait("v", *w)
         return done("v", V.tensor_tensor(out=out, in0=in0, in1=in1, op=op))
 
-    def copyS(out, in_, *w, scale=1.0):
+    def copyS(out, in_, *w, scale=1.0, bias=0.0):
         wait("s", *w)
-        return done("s", S.activation(out=out, in_=in_, func=COPY, scale=scale))
+        return done("s", S.activation(out=out, in_=in_, func=COPY, bias=bias, scale=scale))
 
     def mm(out, lhsT, rhs, start, stop, *w):
         wait("p", *w)
@@ -86,7 +87,7 @@ def rank_program(g, core, T, topo):
         q.dma_start(out=out, in_=in_).then_inc(sem[name], 16)
 
     k_pc = done("gi", g.iota(T.pc[:, 0:1], [[0, 1]], 0, 1))
-    k_i1 = done("gi", g.iota(T.i1[:], [[1, 264]], 128, 0))
+    k_da = done("gi", g.iota(T.da[:], [[1, 264]], 128, -1))
     g.wait_ge(sem.ld, 32)
     fused(T.sm, T.rm, "am")
     g.wait_ge(sem.ld2, 32)
@@ -94,59 +95,45 @@ def rank_program(g, core, T, topo):
     fused(T.sx, T.rx, "ax")
     k_id = done("gi", g.iota(T.win[:, 0:1024], [[1, 1024]], 0, 0, allow_small_or_imprecise_dtypes=True))
 
-    names = ["T", "S", "p", "he", "ho", "r1", "r3", "r9", "r11", "R01", "R03", "u1", "u2", "u9", "u11", "neg", "k7", "g"]
+    names = ["he", "ho", "r7", "r15", "R67", "u1", "u2", "u3", "u4", "T", "wc", "w8", "neg"]
     col = {n: T.cf[:, i:i + 1] for i, n in enumerate(names)}
-    c15, c7, c16b, cn, cn7, cg = [T.ci[:, i:i + 1] for i in range(6)]
+    c15, c7, c16b, cn, cn7 = [T.ci[:, i:i + 1] for i in range(5)]
     k_a1 = done("v", V.memset(T.A1[:], 0))
+    k_w0 = done("v", V.memset(T.W0[:], 0))
     wait("v", k_pc)
-    tsV(c15, T.pc[:, 0:1], 15, A.bitwise_and)
-    tsV(c7, T.pc[:, 0:1], 7, A.bitwise_and)
-    kc = tsV(c16b, T.pc[:, 0:1], 16, A.bitwise_and)
-    kp = copyV(col["p"], T.pc[:, 0:1])
-    kT = tsV(col["T"], c15, 8.0, A.is_lt, kc)
-    tsV(col["he"], c16b, 0.0, A.is_equal)
+    tsV(c16b, T.pc[:, 0:1], 16, A.bitwise_and)
+    kc = tsV(c15, T.pc[:, 0:1], 15, A.bitwise_and)
+    kc7 = tsV(c7, T.pc[:, 0:1], 7, A.bitwise_and)
+    k_db = tsV(T.db[:], T.da[:], 127, A.bitwise_and, k_da)
+    tsV(col["he"], c16b, 0.0, A.is_equal, kc)
     tsV(col["ho"], c16b, 16.0, A.is_equal)
-    tsV(col["r1"], c15, 1.0, A.is_equal)
-    tsV(col["r3"], c15, 3.0, A.is_equal)
-    k = tsV(T.da[:], T.i1[:], col["p"], A.subtract, k_i1, kp)
-    k_db = tsV(T.db[:], T.da[:], 127, A.bitwise_and, k)
-    for i in range(4):
-        k_w0 = tsV(T.W0[:, 256 * i:256 * i + 256], T.i1[:, 0:256], float(256 * i - 128), A.add, kT, s2=col["T"], op1=A.mult)
+    tsV(col["r7"], c15, 7.0, A.is_equal)
     k_mat = tsV(T.WI[:], T.db[:], 0.0, A.is_equal, k_db)
     I = T.WI[:, 0:128]
-    tsV(col["R01"], c7, 2.0, A.is_lt)
-    tsV(col["R03"], c7, 4.0, A.is_lt)
-    tsV(col["r11"], c15, 11.0, A.is_equal)
-    tsV(col["S"], c15, 8.0, A.is_ge)
-    k = tsV(col["r9"], c15, 9.0, A.is_equal)
-    for n, f in (("u1", 6.0), ("u2", 4.0)):
-        tsV(col[n], col["r9"], f, A.mult, k, s2=col["R01"], op1=A.add)
-    tsV(col["u9"], col["r9"], 8.0, A.mult)
-    k = tsV(col["u11"], col["r11"], 8.0, A.mult)
-    tsV(T.D1[:], T.db[:, 0:128], col["u1"], A.is_lt, k)
-    tsV(T.D2[:], T.db[:, 126:254], col["u2"], A.is_lt)
-    tsV(T.D3[:], T.db[:, 0:128], 4.0, A.is_equal, s2=col["R03"], op1=A.mult)
-    tsV(T.B9[:], T.db[:, 1:129], col["u9"], A.is_lt)
-    tsV(T.B11[:], T.db[:, 3:131], col["u11"], A.is_lt)
-    tsV(T.Z8[:], T.db[:, 0:8], 0.0, A.is_lt)
-    kg = tsV(cg, T.pc[:, 0:1], 4, A.arith_shift_right)
+    kr15 = tsV(col["r15"], c15, 15.0, A.is_equal)
+    kr67 = tsV(col["R67"], c7, 6.0, A.is_ge, kc7)
+    wait("v", kr15, kr67)
+    for n, f in (("u1", 2.0), ("u2", 6.0), ("u3", 4.0)):
+        tsV(col[n], col["r15"], f, A.mult, s2=col["R67"], op1=A.add)
+    k = tsV(col["u4"], col["r15"], 8.0, A.mult)
+    k_K1 = tsV(T.K1[:], T.db[:, 2:130], col["u1"], A.is_lt, k)
+    k_B15 = tsV(T.B15[:], T.db[:, 7:135], col["u4"], A.is_lt)
+    tsV(T.E1[:], T.db[:, 6:134], col["u2"], A.is_lt)
+    k_E2 = tsV(T.E2[:], T.db[:, 4:132], col["u3"], A.is_lt)
+    k_T = tsV(col["T"], c15, 8.0, A.is_lt)
+    kk = tsV(T.dr[:], T.db[:, 127:159], 7, A.bitwise_and)
     k = tsV(cn, c15, -1.0, A.mult, s2=128.0, op1=A.add)
-    kk = copyV(col["k7"], c7)
-    kg = copyV(col["g"], cg, kg)
+    kk = tsV(T.OH[:], T.dr[:], 0.0, A.is_equal, kk)
     k = tsV(cn7, cn, 127, A.bitwise_and, k)
-    kk = tsV(T.dq[:], T.i1[:, 0:32], col["k7"], A.subtract, kk)
-    kg = tsV(T.dg[:], T.i1[:, 0:16], col["g"], A.subtract, kg)
-    k = copyV(col["neg"], cn7, k)
-    kk = tsV(T.dr[:], T.dq[:], 7, A.bitwise_and, kk)
-    kg = tsV(T.dh[:], T.dg[:], 7, A.bitwise_and, kg)
-    k_wb = tsV(T.Wb[:], T.db[:, 0:256], col["neg"], A.is_equal, k)
-    k_oh = tsV(T.OH[:], T.dr[:], 1.0, A.is_equal, kk)
-    k_ws = tsV(T.WS[:], T.dh[:], 0.0, A.is_equal, kg, s2=col["S"], op1=A.mult)
+    tsV(col["wc"], col["T"], 1.0 - 2.0 ** -10, A.mult, k_T, s2=2.0 ** -10, op1=A.add)
+    k_neg = copyV(col["neg"], cn7, k)
+    k_oh = tsV(T.OH[:, 0:1], T.OH[:, 0:1], col["T"], A.mult, kk)
+    k_w8 = tsV(col["w8"], col["T"], 8192.0 - 1024.0, A.mult, s2=1024.0, op1=A.add)
+    kcs = tsV(T.cst[:], T.db[:, 0:32], 0.0, A.mult, s2=-1024.0, op1=A.add)
 
     copyS(T.WIe[:], T.WI[:, 0:256], k_mat, scale=col["he"])
     k_wio = copyS(T.WIo[:], T.WI[:, 0:256], scale=col["ho"])
-    k_w1r = copyS(T.W1r[:, 0:255], T.WI[:, 1:256], scale=col["r1"])
-    k_w3r = copyS(T.W3r[:, 0:255], T.WI[:, 3:258], scale=col["r3"])
+    k_w7r = copyS(T.W7r[:, 0:255], T.WI[:, 7:262], scale=col["r7"])
     k_wh = copyS(T.WH[:], T.WI[:, 0:256], scale=1024.0)
 
     nxl, wl = T.rm[:, 0:64, :], T.rm[:, 64:128, :]
@@ -156,22 +143,22 @@ def rank_program(g, core, T, topo):
     Y.dma_start(out=T.cmp[:], in_=nxl).then_inc(sem.cl, 16)
     wait("y", k_a1, k_w0)
     wait("s", k_a1, k_w0)
-    S.dma_start(out=T.W0[9::16, :], in_=wl).then_inc(sem.wl, 16)
-    Y.dma_start(out=T.W0[1::16, :], in_=nxl).then_inc(sem.wl, 16)
-    S.dma_start(out=T.A1[9::16, :], in_=wl).then_inc(sem.wl, 16)
-    Y.dma_start(out=T.A1[8::16, :], in_=wl).then_inc(sem.wl, 16)
+    S.dma_start(out=T.A1[14::16, :], in_=wl).then_inc(sem.al, 16)
+    Y.dma_start(out=T.A1[6::16, :], in_=nxl).then_inc(sem.al, 16)
+    S.dma_start(out=T.A1[15::16, :], in_=wl).then_inc(sem.al, 16)
+    Y.dma_start(out=T.W0[7::16, :], in_=nxl).then_inc(sem.wl, 16)
+    S.dma_start(out=T.W0[15::16, :], in_=wl).then_inc(sem.wl, 16)
     Y.wait_ge(sem.own2, 32)
     Y.wait_ge(sem.ae, N - 1)
     Y.dma_start(out=T.ei[:], in_=T.rre[:]).then_inc(sem.el, 16)
     Y.wait_ge(sem.ax, N - 1)
     Y.dma_start(out=T.xi[:], in_=T.rx[:]).then_inc(sem.xl, 16)
-    k_late = copyS(T.win[:, 0:1024], T.win[:, 0:1024], k_id, scale=col["T"])
-    k_wt = copyS(T.WT[:], T.Wb[:], k_wb, scale=col["T"])
 
     wait("v", ("cl", 16))
     k = copyV(T.c16[:], T.cmp[:])
     wait("v", k)
     k = done("v", V.transpose(out=T.y16[:], in_=T.c16[:]))
+    k_wt = tsV(T.WT[:], T.db[:, 0:256], col["neg"], A.is_equal, k_neg, s2=col["wc"], op1=A.mult)
     wait("p", k, k_wio)
     for b in range(2):
         for h0 in range(2):
@@ -179,149 +166,191 @@ def rank_program(g, core, T, topo):
                 s = 0 if h == h0 else (112 if h == 1 else 16)
                 c = 32 * b + 16 * h
                 kL = mm(T.pR1[:, 2 * b + h0:64:4], (T.WIe, T.WIo)[h0][:, s:s + 128], T.y16[:, c:c + 16], h == 0, h == 1)
-    wait("s", ("wl", 64))
-    k_a16 = copyS(T.a16[:], T.A1[:, VA:1024])
-    wait("v", ("wl", 64))
+    wait("s", ("al", 48))
+    if VA > 512:
+        copyS(T.a16[:, 0:VA - 512], T.A1[:, 512:VA], scale=0.0)
+    k_a16 = copyS(T.a16[:, VA - 512:512], T.A1[:, VA:1024])
+    wait("s", ("wl", 32))
+    wait("v", ("al", 48), ("wl", 32))
     kL1 = copyV(T.L1[:], T.pR1[:, 0:64], kL)
 
-    def relay(out, wide, src, shift, first, *w):
+    def relay(out, wide, src, shift, first, *w, last=True):
         wait("p", *w)
         for r in range(16):
             s = (shift - r) % 128
-            k = mm(out, wide[:, s:s + 128], src[:, r::16], first and r == 0, r == 15)
+            k = mm(out, wide[:, s:s + 128], src[:, r::16], first and r == 0, last and r == 15)
         return k
 
-    pN, pA = (T.pN0, T.pN1), (T.pA0, T.pA1)
+    pN, pA, pK = (T.pN0, T.pN1), (T.pA0, T.pA1), (T.pM1, T.pM0)
     H = (slice(0, 512), slice(512, 1024))
     nA = 1024 - VA
     kg1v = ttV(T.g1[:, 0:VA], T.W0[:].indirect(T.L1[:, 0:VA // 16]), T.A1[:, 0:VA], A.add, kL1)
     kg1s = copyS(T.g1[:, VA:1024], T.W0[:].indirect(T.L1[:, VA // 16:64]), kL1)
-    mm(T.pM0[:, 0:nA], I, T.a16[:], True, False, k_a16)
+    wait("p", k_a16, k_K1, k_B15, k_E2)
+    mm(T.pM0[:, 0:nA], I, T.a16[:, VA - 512:512], True, False)
+    mm(pN[1][:], T.K1[:], T.a16[:], True, False)
+    mm(pA[1][:, 0:VC - 512], T.B15[:], T.a16[:, 0:VC - 512], True, False)
     ka = mm(T.pM0[:, 0:nA], I, T.g1[:, VA:1024], False, True, kg1s)
-    kr = relay(T.pR0[:, 0:64], T.W1r, T.g1, 0, True, k_w1r, kg1v)
+    kr = relay(T.pR0[:, 0:64], T.W7r, T.g1, 0, True, k_w7r, kg1v)
     ks1 = copyS(T.W1[:, VA:1024], T.pM0[:, 0:nA], ka)
     kv1 = copyV(T.W1[:, 0:VA], T.g1[:, 0:VA], kg1v)
     wait("v", ("el", 16))
     klu0 = copyV(T.lu0[:], T.ei[:, 0:32])
     kl = copyV(T.L2[:], T.pR0[:, 0:64], kr)
 
-    mm(pN[0][:], T.D1[:], T.g1[:, H[0]], True, False)
-    mm(pN[1][:], T.D1[:], T.g1[:, H[1]], True, False)
-    mm(pN[1][:, VA - 512:512], T.D1[:], T.a16[:], False, False)
-    mm(pA[0][:], T.B9[:], T.g1[:, H[0]], True, False)
+    kn0 = mm(pN[0][:], T.K1[:], T.g1[:, H[0]], True, True)
+    mm(pN[1][:], T.K1[:], T.g1[:, H[1]], False, False)
+    mm(pK[0][:], T.E1[:], T.g1[:, H[0]], True, False)
+    mm(pK[1][:], T.E1[:], T.a16[:], True, False, ks1)
+    mm(pK[1][:], T.E1[:], T.g1[:, H[1]], False, False)
     kg2v = copyV(T.g2[:, H[0]], T.W1[:].indirect(T.L2[:, 0:32]), kl, ks1, kv1)
     kg2s = copyS(T.g2[:, H[1]], T.W1[:].indirect(T.L2[:, 32:64]), kl, ks1, kv1)
-    m0 = mm(pN[0][:], T.D2[:], T.g2[:, H[0]], False, True, kg2v)
-    m1 = mm(pN[1][:], T.D2[:], T.g2[:, H[1]], False, True, kg2s)
-    kr = relay(T.pR1[:, 0:64], T.W1r, T.g2, 0, True, kL1)
+    kn1 = mm(pN[1][:], I, T.g2[:, H[1]], False, True, kg2s)
+    kr = relay(T.pR1[:, 0:64], T.W7r, T.g2, 0, True, kL1, kg2v)
+    kw2v = ttV(T.W2[:, H[0]], T.g2[:, H[0]], pN[0][:], A.add, kn0, kg2v)
+    copyS(T.mk[:, 0:128], T.OH[:].indirect(T.lu0[:, 0:8]), klu0, k_oh)
+    kw2s = copyS(T.W2[:, H[1]], pN[1][:], kn1)
     k_e16 = copyV(T.e16[:], T.ei[:])
-    kmask = {(0, 0): copyS(T.mk[:, 0:256], T.OH[:].indirect(T.lu0[:, 0:16]), klu0, k_oh)}
-    kw2v = copyV(T.W2[:, H[0]], pN[0][:], m0)
-    kw2s = copyS(T.W2[:, H[1]], pN[1][:], m1)
     kl = copyV(T.L4[:], T.pR1[:, 0:64], kr)
 
-    mm(pA[1][:], T.B9[:], T.g1[:, H[1]], True, False)
-    mm(pA[1][:, VA - 512:512], T.B9[:], T.a16[:], False, False)
-    for h in range(2):
-        mm(pA[h][:], T.B9[:], T.g2[:, H[h]], False, False)
+    ke0 = mm(pK[0][:], T.E2[:], T.g2[:, H[0]], False, True)
+    ke1 = mm(pK[1][:], T.E2[:], T.g2[:, H[1]], False, True)
+    mm(pA[0][:], T.B15[:], T.g1[:, H[0]], True, False)
+    mm(pA[1][:, 0:VC - 512], T.B15[:], T.g1[:, 512:VC], False, False)
+    mm(pA[0][:], T.B15[:], T.g2[:, H[0]], False, False)
+    mm(pA[1][:, 0:VC - 512], T.B15[:], T.g2[:, 512:VC], False, False)
     kg3v = copyV(T.g3[:, H[0]], T.W2[:].indirect(T.L4[:, 0:32]), kl, kw2v, kw2s)
     kg3s = copyS(T.g3[:, H[1]], T.W2[:].indirect(T.L4[:, 32:64]), kl, kw2v, kw2s)
-    m3, kad = [], []
-    for h in range(2):
-        m3.append(mm(pN[h][:], T.D3[:], T.g3[:, H[h]], True, True, (kg3v, kg3s)[h]))
-        kad.append(mm(pA[h][:], T.B11[:], T.g3[:, H[h]], False, True))
-    kr = relay(T.pR0[:, 0:64], T.W3r, T.g3, 0, True, k_w3r, kl)
-    k_h16 = tsV(T.h16[:], T.ei[:], 0.125, A.mult, s2=1024.4375, op1=A.add)
-    kmask[0, 1] = copyS(T.mk[:, 256:512], T.OH[:].indirect(T.lu0[:, 16:32]))
-    ttV(T.win[:, 1024:1536], T.W2[:, H[0]], pN[0][:], A.add, m3[0])
-    kb1 = ttV(T.win[:, 1536:2048], T.W2[:, H[1]], pN[1][:], A.add, m3[1])
-    copyS(T.adF[:, 0:512], pA[0][:], kad[0])
-    kadS = copyS(T.adF[:, 512:VC], pA[1][:, 0:VC - 512], kad[1])
-    kadT = copyS(T.ad16[:, VC:1024], pA[1][:, VC - 512:512], kad[1])
+    kad0 = mm(pA[0][:], T.B15[:], T.g3[:, H[0]], False, True, kg3v)
+    kad1 = mm(pA[1][:, 0:VC - 512], T.B15[:], T.g3[:, 512:VC], False, True, kg3s)
+    kr = relay(T.pR0[:, 0:64], T.W7r, T.g3, 0, True)
+    ttV(T.win[:, 1024:1536], T.g3[:, H[0]], pK[0][:], A.add, ke0, kg3v)
+    kb1 = ttV(T.win[:, 1536:2048], T.g3[:, H[1]], pK[1][:], A.add, ke1, kg3s)
+    kmq = copyS(T.mk[:, 128:256], T.OH[:].indirect(T.lu0[:, 8:16]))
+    k_h16 = copyS(T.h16[:, 0:64], T.ei[:, 0:64], scale=0.125, bias=1024.4375)
+    kx = copyS(T.x16[:], T.xi[:], ("xl", 16))
+    kad = [copyS(T.adF[:, 0:512], pA[0][:], kad0)]
+    kad.append(copyS(T.adF[:, 512:VC], pA[1][:, 0:VC - 512], kad1))
     kl8 = copyV(T.L8[:], T.pR0[:, 0:64], kr)
-    for t in range(1, 8):
-        s = (128 - 16 * t) % 128
-        kt = mm(T.pM1[:, 32 * t:32 * t + 32], T.WI[:, s:s + 128], T.e16[:, 32 * t:32 * t + 32], True, True, k_e16)
+    mm(T.pM0[:, 0:32], T.WH[:, 0:128], T.cst[:], True, False, kcs, k_wh, kb1)
+    mm(T.pM0[:, 0:32], T.WH[:, 0:128], T.h16[:, 0:32], False, False, k_h16)
+    ko = mm(T.pM0[:, 0:32], I, T.x16[:], False, True, kx)
 
-    nS = 1024 - VC
+    parts = ((VC, VB), (VB, 1024))
+    free = {(2, 0): (kw2v, kw2s), (3, 0): (kw2s,), (2, 1): (kad[1],), (3, 1): (kad[1],)}
     kprev = [kb1]
-    kps = [kb1]
     for B in range(2, 5):
         a = 1024 * (B - 1)
         src = T.win[:, a:a + 1024]
-        bank = pN[B % 2]
-        kv = ttV(T.win[:, a + 1024:a + 1024 + VC], src.indirect(T.L8[:, 0:VC // 16]), T.adF[:, 0:VC], A.add, kl8, kadS, *kprev)
-        kg = copyS(T.gb[:, VC:1024], src.indirect(T.L8[:, VC // 16:64]), kl8, kadT, *kprev)
-        mm(bank[:, 0:nS], I, T.ad16[:, VC:1024], True, False, kadT, *kps)
-        km = mm(bank[:, 0:nS], I, T.gb[:, VC:1024], False, True, kg)
-        ks = copyS(T.win[:, a + 1024 + VC:a + 2048], bank[:, 0:nS], km)
-        kprev = [kv, ks]
-        kps = [ks]
+        banks = [(pN[B % 2], pA[B % 2])[n][:, 0:b - u] for n, (u, b) in enumerate(parts)]
+        cuts = (0, 512, VC) if B == 2 else (0, VC)
+        for u0, u1 in zip(cuts, cuts[1:]):
+            kv = ttV(T.win[:, a + 1024 + u0:a + 1024 + u1], src.indirect(T.L8[:, u0 // 16:u1 // 16]), T.adF[:, u0:u1], A.add, kl8, kad[0] if u1 == 512 else kad[1], *kprev)
+        kg, km, ks = [], [], []
+        for u, b in parts:
+            kg.append(copyS(T.gb[:, u:b], src.indirect(T.L8[:, u // 16:b // 16]), kl8, *kprev))
+        for n, (u, b) in enumerate(parts):
+            mm(banks[n], T.B15[:], T.a16[:, u - 512:b - 512], True, False, *free[B, n])
+            for x in (T.g1, T.g2, T.g3):
+                mm(banks[n], T.B15[:], x[:, u:b], False, False)
+        for n, (u, b) in enumerate(parts):
+            km.append(mm(banks[n], I, T.gb[:, u:b], False, True, kg[n]))
+        for n, (u, b) in enumerate(parts):
+            ks.append(copyS(T.win[:, a + 1024 + u:a + 1024 + b], banks[n], km[n]))
+            free[B + 2, n] = (ks[n],)
+        kprev = [kv, ks[1]]
         if B == 2:
-            wait("v", ("xl", 16))
-            kx = copyV(T.x16[:], T.xi[:])
-            mm(T.pR1[:, 0:32], I, T.x16[:], True, False, kx, kl)
-            ko = mm(T.pR1[:, 0:32], T.WH[:, 0:128], T.h16[:, 0:32], False, True, k_h16, k_wh)
-            klu1 = copyV(T.lu[:, 32:64], T.pM1[:, 32:64], kt)
+            wait("p", k_e16)
+            for t in range(1, 8):
+                s = (128 - 16 * t) % 128
+                kt = mm(T.pM1[:, 32 * t:32 * t + 32], T.WI[:, s:s + 128], T.e16[:, 32 * t:32 * t + 32], True, True)
+            koff0 = copyV(T.off[:], T.pM0[:, 0:32], ko)
         if B == 3:
-            koff0 = tsV(T.off[:], T.pR1[:, 0:32], -BIAS, A.add, ko)
+            klu1 = copyV(T.lu[:, 32:64], T.pM1[:, 32:64], kt)
 
-    for z in range(2):
-        mm(pA[z][0:8, 0:256], T.Z8[:], T.g3[:, 0:256], True, False, kadT)
-    Gs, pR = (T.G0, T.G1), (T.pR0, T.pR1)
-    ksum, kgat = {}, {}
+    Gs = (T.G0, T.G1)
+    krel, kgat, kw, kS = {}, {}, {}, {}
     koff = [koff0, koff0]
+    kmask = {(0, 0): kmq}
 
-    def mask(t, k):
-        kmask[t, 0] = kmask[t, 1] = copyS(T.mk[:, 512 * t:512 * t + 512], T.OH[:].indirect(T.lu[:, 32 * t:32 * t + 32]), k)
+    def bank_of(t, z):
+        return ((T.pR0, T.pR1), (T.pM0, T.pM1))[t // 5][z]
+
+    def mask(t, z, k, n=1):
+        l = T.lu0[:, 16 * z:16 * z + 16] if t == 0 else T.lu[:, 32 * t + 16 * z:32 * t + 16 * (z + n)]
+        a = 512 * t + 256 * z
+        kmask[t, z] = kmask[t, z + n - 1] = copyS(T.mk[:, a:a + 256 * n], T.OH[:].indirect(l), k)
 
     def gather(t, z):
         if t > 1:
-            wait("v", ksum[t - 2])
+            wait("v", krel[t - 2, z])
         c = slice(256 * z, 256 * z + 256)
         m = T.mk[:, 512 * t + 256 * z:512 * t + 256 * z + 256]
-        kgat[t, z] = ttV(Gs[t % 2][:, c], T.win[:].indirect(T.off[:, 16 * z:16 * z + 16]), m, A.mult, koff[z], kmask[t, z], k_late, *kprev)
+        kgat[t, z] = ttV(Gs[t % 2][:, c], T.win[:].indirect(T.off[:, 16 * z:16 * z + 16]), m, A.mult, koff[z], kmask[t, z], k_id, *kprev)
 
-    def weights(t):
-        for r in range(16):
-            last = t == 7 and r % 8 == 7
-            ins = P.matmul(out=pA[r // 8][0:8, 32 * (r % 8):32 * (r % 8) + 32], lhsT=T.WS[:, t:t + 8], rhs=Gs[t % 2][:, r::16], start=False, stop=last)
-            if last or r == 15:
-                ksum[t, r] = ksum[t] = done("p", ins)
-
-    mask(1, klu1)
+    mask(0, 1, klu0)
+    mask(1, 0, klu1)
+    mask(1, 1, klu1)
+    k_h16r = copyS(T.h16[:, 64:256], T.ei[:, 64:256], scale=0.125, bias=1024.4375)
     gather(0, 0)
     gather(0, 1)
     klu = copyV(T.lu[:, 64:256], T.pM1[:, 64:256])
-    for t in range(2, 8):
-        mask(t, klu)
-    wait("p", k_wt, k_ws)
-    for t in range(8):
+    mask(2, 0, klu)
+    mask(2, 1, klu)
+    for t in range(3, 8):
+        mask(t, 0, klu, 2)
+    k_wt7 = copyS(T.WT7[:], T.WT[:], k_wt, k_w8, scale=col["w8"])
+    wait("p", k_wt, k_h16)
+    for t in range(7):
         for z in range(2):
-            o = pR[z][:, 0:16]
-            if t < 7:
-                s, c = (128 - 16 * (t + 1)) % 128, 32 * (t + 1) + 16 * z
-                mm(o, T.WH[:, s:s + 128], T.h16[:, c:c + 16], True, False, kl8, koff0, koff[z])
-            elif z == 1:
-                wait("p", kgat[7, 1])
-                weights(7)
-                ktv = copyV(T.OR[0:8, 0:256], pA[0][0:8, 0:256], ksum[7, 7])
-                kts = copyS(T.OR[0:8, 256:512], pA[1][0:8, 0:256], ksum[7, 15])
-            kr = relay(o, T.WT, Gs[t % 2][:, 256 * z:256 * z + 256], 112, t == 7, kgat[t, z], koff[z])
-            if t < 7:
-                koff[z] = tsV(T.off[:, 16 * z:16 * z + 16], o, -BIAS, A.add, kr)
-                gather(t + 1, z)
-            else:
-                koff[z] = copyV(T.OT[:, 16 * z:16 * z + 16], o, kr)
-        if t < 7:
-            weights(t)
+            o = bank_of(t, z)[:, 16 * (t % 5):16 * (t % 5) + 16]
+            if t == 1:
+                wait("p", k_h16r)
+            if t == 5:
+                wait("p", klu)
+            s, c = (128 - 16 * (t + 1)) % 128, 32 * (t + 1) + 16 * z
+            mm(o, T.WH[:, 0:128], T.cst[:, 0:16], True, False, kl8, koff0, koff[z])
+            mm(o, T.WH[:, s:s + 128], T.h16[:, c:c + 16], False, False)
+            krel[t, z] = relay(o, T.WT, Gs[t % 2][:, 256 * z:256 * z + 256], 112, False, kgat[t, z])
+            koff[z] = copyV(T.off[:, 16 * z:16 * z + 16], o, krel[t, z])
+            gather(t + 1, z)
+            if t in (4, 6):
+                b = slice(80 * z, 80 * z + 80) if t == 4 else slice(160 + 32 * z, 192 + 32 * z)
+                k = copyS(T.R1[:, b], bank_of(t, z)[:, 0:b.stop - b.start], koff[z], bias=MAGIC)
+                kS[t, z] = copyS(T.R2[:, b], T.R1[:, b], k, bias=-MAGIC)
+        if t in (5, 6):
+            for z in range(2):
+                b, w = (slice(80 * z, 80 * z + 80), (T.w0, T.w1)[z]) if t == 5 else (slice(160 + 32 * z, 192 + 32 * z), (T.v0, T.v1)[z])
+                kw[t, z] = ttV(w[:], bank_of(0 if t == 5 else 6, z)[:, 0:b.stop - b.start], T.R2[:, b], A.subtract, kS[4 if t == 5 else 6, z])
 
-    wait("s", ktv, kts)
-    S.dma_start(out=T.od[:, 64:128, :], in_=T.OR[0:8, :]).then_inc(sem.st, 16)
-    S.dma_start(out=T.ri[me, 64:128, :], in_=T.OR[me:me + 1, :]).then_inc(sem.own3, 16)
-    wait("y", *koff)
-    Y.dma_start(out=T.od[:, 0:64, :], in_=T.OT[:]).then_inc(sem.st, 16)
-    Y.dma_start(out=T.ri[me, 0:64, :], in_=T.OT[mine, :]).then_inc(sem.own3, 16)
+    wait("p", k_wt7, *kprev)
+    F = T.pA0
+
+    def earlier(z, w, t0, n, k):
+        for t in range(t0, t0 + n):
+            mm(F[:, 16 * z:16 * z + 16], T.WH[:, 16 * (t + 1):16 * (t + 1) + 128], w[:, 16 * (t - t0):16 * (t - t0) + 16], z == 0 and t == 0, False, k)
+
+    earlier(0, T.w0, 0, 5, kw[5, 0])
+    earlier(1, T.w1, 0, 5, kw[5, 1])
+    relay(F[:, 0:16], T.WT7, Gs[1][:, 0:256], 112, False, kgat[7, 0], last=False)
+    wait("p", kgat[7, 1])
+    for r in range(16):
+        s = (112 - r) % 128
+        kf = mm(F[:, 16:32], T.WT7[:, s:s + 128], Gs[1][:, 256 + r:512:16], False, r == 15)
+        if r == 8:
+            earlier(0, T.v0, 5, 2, kw[6, 0])
+        if r == 12:
+            earlier(1, T.v1, 5, 2, kw[6, 1])
+    k8 = tsV(T.OD[:], F[:, 0:32], 8192.0 * MAGIC, A.add, kf, s2=-8192.0 * MAGIC, op1=A.add)
+    kot = ttV(T.OT[:], F[:, 0:32], T.OD[:], A.subtract, k8)
+    kol = copyS(T.OL[:], T.OD[:], k8, scale=2.0 ** -13)
+
+    wait("y", kot)
+    Y.dma_start(out=T.od[:, 64:128, :], in_=T.OT[:]).then_inc(sem.st, 16)
+    Y.dma_start(out=T.ri[me, 64:128, :], in_=T.OT[mine, :]).then_inc(sem.own3, 16)
+    wait("s", kol)
+    S.dma_start(out=T.od[:, 0:64, :], in_=T.OL[:]).then_inc(sem.st, 16)
+    S.dma_start(out=T.ri[me, 0:64, :], in_=T.OL[mine, :]).then_inc(sem.own3, 16)
     g.wait_ge(sem.st, 32)
     fused(T.od, T.ri, "ar")
     for e in (Y, S):

from concourse.bass import DstId, RemoteDMATransfer
from concourse.mybir import AluOpType, ActivationFunctionType

VA = 576
VC = 736
VB = 896
MAGIC = 1.5 * 2.0 ** 23
SCRATCH = {"OH": ("sbuf", [128, 32], "float32"), "mk": ("sbuf", [128, 4096], "bfloat16")}
for _n, _w in (("sm", 16), ("rm", 16), ("se", 32), ("rre", 32), ("sx", 4), ("rx", 4)):
    SCRATCH[_n] = ("dram", [8, 128, _w], "int32")
for _n in ("od", "ri"):
    SCRATCH[_n] = ("dram", [8, 128, 8], "float32")
for _d, _l in (("int32", "W0:1024 A1:1024 cmp:64 ei:256 xi:32 pc:1 ci:8 da:264 db:264 dr:32"),
               ("float32", "win:5120 W1:1024 W2:1024 adF:1024 OL:32 OD:32 OT:32 cf:24 R1:224 R2:224"),
               ("float16", "g1:1024 g2:1024 g3:1024 a16:512 gb:1024 c16:64 y16:64 e16:256 h16:256 x16:32 G0:512 G1:512 K1:128 E1:128 E2:128 B15:128 WI:264 WIe:256 WIo:256 WH:256 W7r:256 WT:256 WT7:256 cst:32 w0:80 w1:80 v0:32 v1:32"),
               ("uint16", "L1:64 L2:64 L4:64 L8:64 lu0:32 lu:256 off:32")):
    for _e in _l.split():
        SCRATCH[_e.split(":")[0]] = ("sbuf", [128, int(_e.split(":")[1])], _d)
for _n in ("pR0", "pR1", "pM0", "pM1", "pN0", "pN1", "pA0", "pA1"):
    SCRATCH[_n] = ("psum", [128, 512], "float32")
SEMAPHORES = ["ld", "own", "ld2", "own2", "am", "ae", "ax", "cl", "wl", "al", "el", "xl", "v", "s", "p", "gi", "ls", "st", "own3", "ar", "fin"]


def rank_program(g, core, T, topo):
    me = T.rank_of(core)
    if me is None:
        return
    V, S, P, Y = g.vector, g.scalar, g.tensor, g.sync
    A = AluOpType
    COPY = ActivationFunctionType.Copy
    N = len(T.cores)
    others = [(me + d) % N for d in range(1, N)]
    sem = T.sem
    cnt = {"v": 0, "s": 0, "p": 0, "gi": 0}
    seen = {}
    queues = {"v": V, "s": S, "p": P, "g": g, "y": Y}

    def wait(q, *toks):
        for name, n in toks:
            if n > seen.get((q, name), 0):
                queues[q].wait_ge(sem[name], n)
                seen[(q, name)] = n

    def done(name, ins):
        cnt[name] += 1
        ins.then_inc(sem[name], 1)
        return (name, cnt[name])

    def copyV(out, in_, *w):
        wait("v", *w)
        return done("v", V.tensor_copy(out=out, in_=in_))

    def tsV(out, in0, s1, op0, *w, s2=None, op1=None):
        wait("v", *w)
        if op1 is None:
            return done("v", V.tensor_scalar(out=out, in0=in0, scalar1=s1, scalar2=None, op0=op0))
        return done("v", V.tensor_scalar(out=out, in0=in0, scalar1=s1, scalar2=s2, op0=op0, op1=op1))

    def ttV(out, in0, in1, op, *w):
        wait("v", *w)
        return done("v", V.tensor_tensor(out=out, in0=in0, in1=in1, op=op))

    def copyS(out, in_, *w, scale=1.0, bias=0.0):
        wait("s", *w)
        return done("s", S.activation(out=out, in_=in_, func=COPY, bias=bias, scale=scale))

    def mm(out, lhsT, rhs, start, stop, *w):
        wait("p", *w)
        ins = P.matmul(out=out, lhsT=lhsT, rhs=rhs, start=start, stop=stop)
        return done("p", ins) if stop else None

    def fused(src, dst, rsem):
        tr = []
        for n, d in enumerate(others):
            c = T.cores[d]
            rid, pid, _ = topo.addr(c)
            eng = topo.engines(core, c)
            e = eng[(2 * n) % len(eng)]
            tr.append(RemoteDMATransfer(src=src[d], dst=dst[me], dst_ids=[DstId(rid=rid, pnc=pid)], dma_engine_mask=1 << e, remote_sem=sem[rsem]))
        g.remote_dma_fused(tr, local_sem=sem.ls)

    mine = slice(16 * me, 16 * me + 16)
    for q, out, in_, name in ((Y, T.sm[:, 0:64, :], T.nx[:, :], "ld"), (S, T.sm[:, 64:128, :], T.w[:, :], "ld"),
                              (Y, T.se[:], T.e[:, :], "ld2"), (S, T.sx[:], T.x[:, :], "ld2"),
                              (Y, T.rm[me, 0:64, :], T.nx[me, :], "own"), (S, T.rm[me, 64:128, :], T.w[me, :], "own"),
                              (Y, T.rre[me], T.e[mine, :], "own2"), (S, T.rx[me], T.x[mine, :], "own2")):
        q.dma_start(out=out, in_=in_).then_inc(sem[name], 16)

    k_pc = done("gi", g.iota(T.pc[:, 0:1], [[0, 1]], 0, 1))
    k_da = done("gi", g.iota(T.da[:], [[1, 264]], 128, -1))
    g.wait_ge(sem.ld, 32)
    fused(T.sm, T.rm, "am")
    g.wait_ge(sem.ld2, 32)
    fused(T.se, T.rre, "ae")
    fused(T.sx, T.rx, "ax")
    k_id = done("gi", g.iota(T.win[:, 0:1024], [[1, 1024]], 0, 0, allow_small_or_imprecise_dtypes=True))

    names = ["he", "ho", "r7", "r15", "R67", "u1", "u2", "u3", "u4", "T", "wc", "w8", "neg"]
    col = {n: T.cf[:, i:i + 1] for i, n in enumerate(names)}
    c15, c7, c16b, cn, cn7 = [T.ci[:, i:i + 1] for i in range(5)]
    k_a1 = done("v", V.memset(T.A1[:], 0))
    k_w0 = done("v", V.memset(T.W0[:], 0))
    wait("v", k_pc)
    tsV(c16b, T.pc[:, 0:1], 16, A.bitwise_and)
    kc = tsV(c15, T.pc[:, 0:1], 15, A.bitwise_and)
    kc7 = tsV(c7, T.pc[:, 0:1], 7, A.bitwise_and)
    k_db = tsV(T.db[:], T.da[:], 127, A.bitwise_and, k_da)
    tsV(col["he"], c16b, 0.0, A.is_equal, kc)
    tsV(col["ho"], c16b, 16.0, A.is_equal)
    tsV(col["r7"], c15, 7.0, A.is_equal)
    k_mat = tsV(T.WI[:], T.db[:], 0.0, A.is_equal, k_db)
    I = T.WI[:, 0:128]
    kr15 = tsV(col["r15"], c15, 15.0, A.is_equal)
    kr67 = tsV(col["R67"], c7, 6.0, A.is_ge, kc7)
    wait("v", kr15, kr67)
    for n, f in (("u1", 2.0), ("u2", 6.0), ("u3", 4.0)):
        tsV(col[n], col["r15"], f, A.mult, s2=col["R67"], op1=A.add)
    k = tsV(col["u4"], col["r15"], 8.0, A.mult)
    k_K1 = tsV(T.K1[:], T.db[:, 2:130], col["u1"], A.is_lt, k)
    k_B15 = tsV(T.B15[:], T.db[:, 7:135], col["u4"], A.is_lt)
    tsV(T.E1[:], T.db[:, 6:134], col["u2"], A.is_lt)
    k_E2 = tsV(T.E2[:], T.db[:, 4:132], col["u3"], A.is_lt)
    k_T = tsV(col["T"], c15, 8.0, A.is_lt)
    kk = tsV(T.dr[:], T.db[:, 127:159], 7, A.bitwise_and)
    k = tsV(cn, c15, -1.0, A.mult, s2=128.0, op1=A.add)
    kk = tsV(T.OH[:], T.dr[:], 0.0, A.is_equal, kk)
    k = tsV(cn7, cn, 127, A.bitwise_and, k)
    tsV(col["wc"], col["T"], 1.0 - 2.0 ** -10, A.mult, k_T, s2=2.0 ** -10, op1=A.add)
    k_neg = copyV(col["neg"], cn7, k)
    k_oh = tsV(T.OH[:, 0:1], T.OH[:, 0:1], col["T"], A.mult, kk)
    k_w8 = tsV(col["w8"], col["T"], 8192.0 - 1024.0, A.mult, s2=1024.0, op1=A.add)
    kcs = tsV(T.cst[:], T.db[:, 0:32], 0.0, A.mult, s2=-1024.0, op1=A.add)

    copyS(T.WIe[:], T.WI[:, 0:256], k_mat, scale=col["he"])
    k_wio = copyS(T.WIo[:], T.WI[:, 0:256], scale=col["ho"])
    k_w7r = copyS(T.W7r[:, 0:255], T.WI[:, 7:262], scale=col["r7"])
    k_wh = copyS(T.WH[:], T.WI[:, 0:256], scale=1024.0)

    nxl, wl = T.rm[:, 0:64, :], T.rm[:, 64:128, :]
    for e in (Y, S):
        e.wait_ge(sem.own, 32)
        e.wait_ge(sem.am, N - 1)
    Y.dma_start(out=T.cmp[:], in_=nxl).then_inc(sem.cl, 16)
    wait("y", k_a1, k_w0)
    wait("s", k_a1, k_w0)
    S.dma_start(out=T.A1[14::16, :], in_=wl).then_inc(sem.al, 16)
    Y.dma_start(out=T.A1[6::16, :], in_=nxl).then_inc(sem.al, 16)
    S.dma_start(out=T.A1[15::16, :], in_=wl).then_inc(sem.al, 16)
    Y.dma_start(out=T.W0[7::16, :], in_=nxl).then_inc(sem.wl, 16)
    S.dma_start(out=T.W0[15::16, :], in_=wl).then_inc(sem.wl, 16)
    Y.wait_ge(sem.own2, 32)
    Y.wait_ge(sem.ae, N - 1)
    Y.dma_start(out=T.ei[:], in_=T.rre[:]).then_inc(sem.el, 16)
    Y.wait_ge(sem.ax, N - 1)
    Y.dma_start(out=T.xi[:], in_=T.rx[:]).then_inc(sem.xl, 16)

    wait("v", ("cl", 16))
    k = copyV(T.c16[:], T.cmp[:])
    wait("v", k)
    k = done("v", V.transpose(out=T.y16[:], in_=T.c16[:]))
    k_wt = tsV(T.WT[:], T.db[:, 0:256], col["neg"], A.is_equal, k_neg, s2=col["wc"], op1=A.mult)
    wait("p", k, k_wio)
    for b in range(2):
        for h0 in range(2):
            for h in range(2):
                s = 0 if h == h0 else (112 if h == 1 else 16)
                c = 32 * b + 16 * h
                kL = mm(T.pR1[:, 2 * b + h0:64:4], (T.WIe, T.WIo)[h0][:, s:s + 128], T.y16[:, c:c + 16], h == 0, h == 1)
    wait("s", ("al", 48))
    if VA > 512:
        copyS(T.a16[:, 0:VA - 512], T.A1[:, 512:VA], scale=0.0)
    k_a16 = copyS(T.a16[:, VA - 512:512], T.A1[:, VA:1024])
    wait("s", ("wl", 32))
    wait("v", ("al", 48), ("wl", 32))
    kL1 = copyV(T.L1[:], T.pR1[:, 0:64], kL)

    def relay(out, wide, src, shift, first, *w, last=True):
        wait("p", *w)
        for r in range(16):
            s = (shift - r) % 128
            k = mm(out, wide[:, s:s + 128], src[:, r::16], first and r == 0, last and r == 15)
        return k

    pN, pA, pK = (T.pN0, T.pN1), (T.pA0, T.pA1), (T.pM1, T.pM0)
    H = (slice(0, 512), slice(512, 1024))
    nA = 1024 - VA
    kg1v = ttV(T.g1[:, 0:VA], T.W0[:].indirect(T.L1[:, 0:VA // 16]), T.A1[:, 0:VA], A.add, kL1)
    kg1s = copyS(T.g1[:, VA:1024], T.W0[:].indirect(T.L1[:, VA // 16:64]), kL1)
    wait("p", k_a16, k_K1, k_B15, k_E2)
    mm(T.pM0[:, 0:nA], I, T.a16[:, VA - 512:512], True, False)
    mm(pN[1][:], T.K1[:], T.a16[:], True, False)
    mm(pA[1][:, 0:VC - 512], T.B15[:], T.a16[:, 0:VC - 512], True, False)
    ka = mm(T.pM0[:, 0:nA], I, T.g1[:, VA:1024], False, True, kg1s)
    kr = relay(T.pR0[:, 0:64], T.W7r, T.g1, 0, True, k_w7r, kg1v)
    ks1 = copyS(T.W1[:, VA:1024], T.pM0[:, 0:nA], ka)
    kv1 = copyV(T.W1[:, 0:VA], T.g1[:, 0:VA], kg1v)
    wait("v", ("el", 16))
    klu0 = copyV(T.lu0[:], T.ei[:, 0:32])
    kl = copyV(T.L2[:], T.pR0[:, 0:64], kr)

    kn0 = mm(pN[0][:], T.K1[:], T.g1[:, H[0]], True, True)
    mm(pN[1][:], T.K1[:], T.g1[:, H[1]], False, False)
    mm(pK[0][:], T.E1[:], T.g1[:, H[0]], True, False)
    mm(pK[1][:], T.E1[:], T.a16[:], True, False, ks1)
    mm(pK[1][:], T.E1[:], T.g1[:, H[1]], False, False)
    kg2v = copyV(T.g2[:, H[0]], T.W1[:].indirect(T.L2[:, 0:32]), kl, ks1, kv1)
    kg2s = copyS(T.g2[:, H[1]], T.W1[:].indirect(T.L2[:, 32:64]), kl, ks1, kv1)
    kn1 = mm(pN[1][:], I, T.g2[:, H[1]], False, True, kg2s)
    kr = relay(T.pR1[:, 0:64], T.W7r, T.g2, 0, True, kL1, kg2v)
    kw2v = ttV(T.W2[:, H[0]], T.g2[:, H[0]], pN[0][:], A.add, kn0, kg2v)
    copyS(T.mk[:, 0:128], T.OH[:].indirect(T.lu0[:, 0:8]), klu0, k_oh)
    kw2s = copyS(T.W2[:, H[1]], pN[1][:], kn1)
    k_e16 = copyV(T.e16[:], T.ei[:])
    kl = copyV(T.L4[:], T.pR1[:, 0:64], kr)

    ke0 = mm(pK[0][:], T.E2[:], T.g2[:, H[0]], False, True)
    ke1 = mm(pK[1][:], T.E2[:], T.g2[:, H[1]], False, True)
    mm(pA[0][:], T.B15[:], T.g1[:, H[0]], True, False)
    mm(pA[1][:, 0:VC - 512], T.B15[:], T.g1[:, 512:VC], False, False)
    mm(pA[0][:], T.B15[:], T.g2[:, H[0]], False, False)
    mm(pA[1][:, 0:VC - 512], T.B15[:], T.g2[:, 512:VC], False, False)
    kg3v = copyV(T.g3[:, H[0]], T.W2[:].indirect(T.L4[:, 0:32]), kl, kw2v, kw2s)
    kg3s = copyS(T.g3[:, H[1]], T.W2[:].indirect(T.L4[:, 32:64]), kl, kw2v, kw2s)
    kad0 = mm(pA[0][:], T.B15[:], T.g3[:, H[0]], False, True, kg3v)
    kad1 = mm(pA[1][:, 0:VC - 512], T.B15[:], T.g3[:, 512:VC], False, True, kg3s)
    kr = relay(T.pR0[:, 0:64], T.W7r, T.g3, 0, True)
    ttV(T.win[:, 1024:1536], T.g3[:, H[0]], pK[0][:], A.add, ke0, kg3v)
    kb1 = ttV(T.win[:, 1536:2048], T.g3[:, H[1]], pK[1][:], A.add, ke1, kg3s)
    kmq = copyS(T.mk[:, 128:256], T.OH[:].indirect(T.lu0[:, 8:16]))
    k_h16 = copyS(T.h16[:, 0:64], T.ei[:, 0:64], scale=0.125, bias=1024.4375)
    kx = copyS(T.x16[:], T.xi[:], ("xl", 16))
    kad = [copyS(T.adF[:, 0:512], pA[0][:], kad0)]
    kad.append(copyS(T.adF[:, 512:VC], pA[1][:, 0:VC - 512], kad1))
    kl8 = copyV(T.L8[:], T.pR0[:, 0:64], kr)
    mm(T.pM0[:, 0:32], T.WH[:, 0:128], T.cst[:], True, False, kcs, k_wh, kb1)
    mm(T.pM0[:, 0:32], T.WH[:, 0:128], T.h16[:, 0:32], False, False, k_h16)
    ko = mm(T.pM0[:, 0:32], I, T.x16[:], False, True, kx)

    parts = ((VC, VB), (VB, 1024))
    free = {(2, 0): (kw2v, kw2s), (3, 0): (kw2s,), (2, 1): (kad[1],), (3, 1): (kad[1],)}
    kprev = [kb1]
    for B in range(2, 5):
        a = 1024 * (B - 1)
        src = T.win[:, a:a + 1024]
        banks = [(pN[B % 2], pA[B % 2])[n][:, 0:b - u] for n, (u, b) in enumerate(parts)]
        cuts = (0, 512, VC) if B == 2 else (0, VC)
        for u0, u1 in zip(cuts, cuts[1:]):
            kv = ttV(T.win[:, a + 1024 + u0:a + 1024 + u1], src.indirect(T.L8[:, u0 // 16:u1 // 16]), T.adF[:, u0:u1], A.add, kl8, kad[0] if u1 == 512 else kad[1], *kprev)
        kg, km, ks = [], [], []
        for u, b in parts:
            kg.append(copyS(T.gb[:, u:b], src.indirect(T.L8[:, u // 16:b // 16]), kl8, *kprev))
        for n, (u, b) in enumerate(parts):
            mm(banks[n], T.B15[:], T.a16[:, u - 512:b - 512], True, False, *free[B, n])
            for x in (T.g1, T.g2, T.g3):
                mm(banks[n], T.B15[:], x[:, u:b], False, False)
        for n, (u, b) in enumerate(parts):
            km.append(mm(banks[n], I, T.gb[:, u:b], False, True, kg[n]))
        for n, (u, b) in enumerate(parts):
            ks.append(copyS(T.win[:, a + 1024 + u:a + 1024 + b], banks[n], km[n]))
            free[B + 2, n] = (ks[n],)
        kprev = [kv, ks[1]]
        if B == 2:
            wait("p", k_e16)
            for t in range(1, 8):
                s = (128 - 16 * t) % 128
                kt = mm(T.pM1[:, 32 * t:32 * t + 32], T.WI[:, s:s + 128], T.e16[:, 32 * t:32 * t + 32], True, True)
            koff0 = copyV(T.off[:], T.pM0[:, 0:32], ko)
        if B == 3:
            klu1 = copyV(T.lu[:, 32:64], T.pM1[:, 32:64], kt)

    Gs = (T.G0, T.G1)
    krel, kgat, kw, kS = {}, {}, {}, {}
    koff = [koff0, koff0]
    kmask = {(0, 0): kmq}

    def bank_of(t, z):
        return ((T.pR0, T.pR1), (T.pM0, T.pM1))[t // 5][z]

    def mask(t, z, k, n=1):
        l = T.lu0[:, 16 * z:16 * z + 16] if t == 0 else T.lu[:, 32 * t + 16 * z:32 * t + 16 * (z + n)]
        a = 512 * t + 256 * z
        kmask[t, z] = kmask[t, z + n - 1] = copyS(T.mk[:, a:a + 256 * n], T.OH[:].indirect(l), k)

    def gather(t, z):
        if t > 1:
            wait("v", krel[t - 2, z])
        c = slice(256 * z, 256 * z + 256)
        m = T.mk[:, 512 * t + 256 * z:512 * t + 256 * z + 256]
        kgat[t, z] = ttV(Gs[t % 2][:, c], T.win[:].indirect(T.off[:, 16 * z:16 * z + 16]), m, A.mult, koff[z], kmask[t, z], k_id, *kprev)

    mask(0, 1, klu0)
    mask(1, 0, klu1)
    mask(1, 1, klu1)
    k_h16r = copyS(T.h16[:, 64:256], T.ei[:, 64:256], scale=0.125, bias=1024.4375)
    gather(0, 0)
    gather(0, 1)
    klu = copyV(T.lu[:, 64:256], T.pM1[:, 64:256])
    mask(2, 0, klu)
    mask(2, 1, klu)
    for t in range(3, 8):
        mask(t, 0, klu, 2)
    k_wt7 = copyS(T.WT7[:], T.WT[:], k_wt, k_w8, scale=col["w8"])
    wait("p", k_wt, k_h16)
    for t in range(7):
        for z in range(2):
            o = bank_of(t, z)[:, 16 * (t % 5):16 * (t % 5) + 16]
            if t == 1:
                wait("p", k_h16r)
            if t == 5:
                wait("p", klu)
            s, c = (128 - 16 * (t + 1)) % 128, 32 * (t + 1) + 16 * z
            mm(o, T.WH[:, 0:128], T.cst[:, 0:16], True, False, kl8, koff0, koff[z])
            mm(o, T.WH[:, s:s + 128], T.h16[:, c:c + 16], False, False)
            krel[t, z] = relay(o, T.WT, Gs[t % 2][:, 256 * z:256 * z + 256], 112, False, kgat[t, z])
            koff[z] = copyV(T.off[:, 16 * z:16 * z + 16], o, krel[t, z])
            gather(t + 1, z)
            if t in (4, 6):
                b = slice(80 * z, 80 * z + 80) if t == 4 else slice(160 + 32 * z, 192 + 32 * z)
                k = copyS(T.R1[:, b], bank_of(t, z)[:, 0:b.stop - b.start], koff[z], bias=MAGIC)
                kS[t, z] = copyS(T.R2[:, b], T.R1[:, b], k, bias=-MAGIC)
        if t in (5, 6):
            for z in range(2):
                b, w = (slice(80 * z, 80 * z + 80), (T.w0, T.w1)[z]) if t == 5 else (slice(160 + 32 * z, 192 + 32 * z), (T.v0, T.v1)[z])
                kw[t, z] = ttV(w[:], bank_of(0 if t == 5 else 6, z)[:, 0:b.stop - b.start], T.R2[:, b], A.subtract, kS[4 if t == 5 else 6, z])

    wait("p", k_wt7, *kprev)
    F = T.pA0

    def earlier(z, w, t0, n, k):
        for t in range(t0, t0 + n):
            mm(F[:, 16 * z:16 * z + 16], T.WH[:, 16 * (t + 1):16 * (t + 1) + 128], w[:, 16 * (t - t0):16 * (t - t0) + 16], z == 0 and t == 0, False, k)

    earlier(0, T.w0, 0, 5, kw[5, 0])
    earlier(1, T.w1, 0, 5, kw[5, 1])
    relay(F[:, 0:16], T.WT7, Gs[1][:, 0:256], 112, False, kgat[7, 0], last=False)
    wait("p", kgat[7, 1])
    for r in range(16):
        s = (112 - r) % 128
        kf = mm(F[:, 16:32], T.WT7[:, s:s + 128], Gs[1][:, 256 + r:512:16], False, r == 15)
        if r == 8:
            earlier(0, T.v0, 5, 2, kw[6, 0])
        if r == 12:
            earlier(1, T.v1, 5, 2, kw[6, 1])
    k8 = tsV(T.OD[:], F[:, 0:32], 8192.0 * MAGIC, A.add, kf, s2=-8192.0 * MAGIC, op1=A.add)
    kot = ttV(T.OT[:], F[:, 0:32], T.OD[:], A.subtract, k8)
    kol = copyS(T.OL[:], T.OD[:], k8, scale=2.0 ** -13)

    wait("y", kot)
    Y.dma_start(out=T.od[:, 64:128, :], in_=T.OT[:]).then_inc(sem.st, 16)
    Y.dma_start(out=T.ri[me, 64:128, :], in_=T.OT[mine, :]).then_inc(sem.own3, 16)
    wait("s", kol)
    S.dma_start(out=T.od[:, 0:64, :], in_=T.OL[:]).then_inc(sem.st, 16)
    S.dma_start(out=T.ri[me, 0:64, :], in_=T.OL[mine, :]).then_inc(sem.own3, 16)
    g.wait_ge(sem.st, 32)
    fused(T.od, T.ri, "ar")
    for e in (Y, S):
        e.wait_ge(sem.own3, 32)
        e.wait_ge(sem.ar, N - 1)
    Y.dma_start(out=T.last[:, :], in_=T.ri[:, 0:64, :]).then_inc(sem.fin, 16)
    S.dma_start(out=T.total[:, :], in_=T.ri[:, 64:128, :]).then_inc(sem.fin, 16)
    wait("g", ("v", cnt["v"]), ("s", cnt["s"]), ("p", cnt["p"]), ("gi", cnt["gi"]))
    g.wait_ge(sem.ls, 4 * (N - 1))
    g.wait_ge(sem.fin, 32)
